import numpy as np, ml_dtypes
CORES = [6,15,38,47]
N = 4
import mx_ref
BF = ml_dtypes.bfloat16
def gentries(a):
    return np.ascontiguousarray(a.reshape(8, 16, -1).transpose(0, 2, 1)).reshape(8, -1)
def gtable(e):
    e = np.asarray(e); return np.ascontiguousarray(e.reshape(8, -1, 16).transpose(0, 2, 1)).reshape(128, -1).astype(np.int32)
def gcols(t, e):
    v = np.concatenate([t.reshape(8, 16, -1, 4), np.zeros((8, 16, 1, 4), BF)], axis=2)
    return np.ascontiguousarray(np.stack([v[g][:, e[g]] for g in range(8)])).reshape(128, -1)
def tile(rs):
    return np.stack(rs, axis=2).reshape(128, -1).astype(BF)
def pick(q, e):
    c = np.concatenate([q[0].reshape(128, -1, 4), np.zeros((128, 1, 4), np.uint8)], axis=1); s = np.concatenate([q[1], np.ones((16, 1), np.uint8)], axis=1)
    return (np.ascontiguousarray(c[:, e].reshape(128, -1)), np.ascontiguousarray(s[:, e]))
def join(*qs):
    return (np.concatenate([q[0] for q in qs], axis=1), np.concatenate([q[1] for q in qs], axis=1))
def put(q, e, v):
    c, s = q[0].reshape(128, -1, 4).copy(), q[1].copy(); c[:, e] = v[0].reshape(128, -1, 4); s[:, e] = v[1]
    return (c.reshape(128, -1), s)
def pk(c, s):
    return (np.ascontiguousarray(c), mx_ref.live(s))
def emit(q):
    return q[0], q[1]
def packed(v, rng):
    q = [mx_ref.quantize(np.ascontiguousarray(v[r])) for r in range(N)]
    return np.stack([a for a, b in q]), np.stack([mx_ref.plane(b, rng) for a, b in q])
def values_of_codes():
    e, c = np.zeros((128, 128, 4), np.float32), np.zeros((128, 2, 4), np.uint8)
    e[np.arange(128), np.arange(128), 0] = 1
    c[:127, :, 0] = np.arange(256).reshape(2, 128).T[:127]
    return mx_ref.matmul(mx_ref.quantize(e.reshape(128, 512).astype(BF)), (c.reshape(128, 8), np.full((16, 2), 127, np.uint8))).T.reshape(-1).astype(np.float64)
CODE_VALUE, SCALE_VALUE = values_of_codes(), 2.0 ** (np.arange(256) - 127.0)
def decode(q):
    return (CODE_VALUE[q[0]].reshape(16, 8, -1, 4) * SCALE_VALUE[q[1]][:, None, :, None] + 0.0).reshape(128, -1).astype(np.float32)
def f(rng, *shape):
    return mx_ref.flush((rng.standard_normal(shape, dtype=np.float32) * np.exp2(rng.integers(-2, 3, shape[:-1] + (1,)))).astype(BF))
def wide(rng, *shape, cols=0):
    v = rng.standard_normal(shape, dtype=np.float32) * np.exp2(rng.integers(-12, 13, shape)).astype(np.float32)
    if cols: v *= np.repeat(np.exp2(rng.integers(-cols, cols + 1, shape[:-2] + (1, shape[-1] // 4))) * (rng.random(shape[:-2] + (1, shape[-1] // 4)) > 0.0625), 4, axis=-1).astype(np.float32)
    return mx_ref.flush(v.astype(BF))
C, T = 512, 224
STEPS = [1, 2, 3]
def big(v):
    v = v.astype(np.float32)
    v[np.abs(v) < np.float32(2.0 ** -16)] = 0
    return v.astype(BF)
def numbers_of(rng):
    return {"x": big(f(rng, N, 128, 4 * C)), "u": np.array(f(rng, N, 128, 512)), "v": np.array(f(rng, N, 128, 512))}
def lists(rng, a=None):
    if a is None: a = np.argsort(rng.random((N, 8, C // 8, 8)), axis=3)
    a = (a + 8 * np.arange(C // 8)[:, None]).reshape(N, 8, C)
    c = np.argsort(rng.random((N, 8, C)), axis=2)
    return {"p": np.stack([gtable(a[r]) for r in range(N)]), "h": np.stack([gtable(c[r]) for r in range(N)])}
def weights(rng, w):
    c, s = packed(np.ascontiguousarray(w).reshape(N, 128, 2048), rng)
    return {"wc": c, "ws": s}
def layers(rng, still=[]):
    w = big(f(rng, N, 128, 2048)).reshape(N, 8, 16, 4, 8, 16, 4)
    for i in still:
        w[:, :, i] = 0
        w[:, :, :, :, :, i] = 0
    return weights(rng, w)
def setup_inputs(rng):
    return {**numbers_of(rng), **lists(rng), **layers(rng)}
def setup_inputs_ties(rng):
    d = numbers_of(rng)
    x = d["x"].astype(np.float32).reshape(N, 8, 16, C, 4)
    x[:, :, 0] = 0
    x[:, :, 0, :, 0] = rng.integers(-2, 3, (N, 8, C))
    z = np.exp2(rng.integers(-14, -7, (N, 8, C, 32))) * (1 + (2 * rng.integers(0, 64, (N, 8, C, 32)) + 1) / 128) * rng.choice([-1.0, 1.0], (N, 8, C, 32))
    np.put_along_axis(z, rng.integers(0, 32, (N, 8, C, 1)), 1.96875 * rng.choice([-1.0, 1.0], (N, 8, C, 1)), axis=3)
    z = z * np.exp2(rng.integers(-2, 3, (N, 8, C, 1)))
    x[:, :, 8:] = z.reshape(N, 8, C, 8, 4).transpose(0, 1, 3, 2, 4)
    u = d["u"].reshape(N, 128, 128, 4)
    u[:, :, ::16] = 0
    o = rng.permutation(N)
    for r in range(N):
        for i in range(0, 128, 16): u[r, i, i, 0] = 0.0 if r == o[0] else -1.0 if r == o[1] else 1.0
    return {"x": x.reshape(N, 128, 4 * C).astype(BF), "u": u.reshape(N, 128, 512), "v": d["v"], **lists(rng), **layers(rng, [0, 8, 9, 10, 11, 12, 13, 14, 15])}
def setup_inputs_near(rng):
    d = numbers_of(rng)
    x = d["x"].astype(np.float32).reshape(N, 8, 16, C, 4)
    u = d["u"].reshape(N, 128, 128, 4)
    x[:, :, 0] = 0
    x[:, :, 8:] = 0
    u[:, :, ::16] = 0
    s = rng.integers(0, 16, (N, 8, C))
    k = rng.permutation(8) % 4
    for g in range(8):
        i = 16 * g
        if k[g] < 2:
            x[:, g, 0, :, 0] = 1
            x[:, g, 8] = ((s[:, g, :, None] >> np.arange(4)) & 1) * np.exp2(np.arange(4) - 23.0)
            x[:, g, 11, :, 0] = 2.0 ** -10
            c = 1.0 if k[g] == 0 else -2.0 ** -30
            u[:, i, i, 0] = c
            u[:, i + 8, i] = c
            u[:, i + 11, i, 0] = c
        else:
            x[:, g, 10, :, 0] = (1 + s[:, g] % 8 * 0.125) * 2.0 ** -30
            u[:, i + 10, i, 0] = 2.0 ** -30 if k[g] == 2 else -2.0 ** -30
            if k[g] == 3: x[np.arange(N), g, 10, rng.integers(0, C, N), 0] = 2.0 ** 30
    return {"x": x.reshape(N, 128, 4 * C).astype(BF), "u": u.reshape(N, 128, 512), "v": d["v"], **lists(rng), **layers(rng, [0, 8, 9, 10, 11, 12, 13, 14, 15])}
def setup_inputs_huge(rng):
    d = numbers_of(rng)
    o = rng.permutation(N)
    x = 0.6 + 0.4 * rng.random((N, 8, 16, C, 4))
    x[o == 0] = 0.875 + 0.25 * (x[o == 0] - 0.5)
    c = rng.choice([-1.0, 1.0], (N, 1, 1, C, 1))
    c[o % 2 == 0] = -1
    u = d["u"].reshape(N, 128, 128, 4)
    a = 1 - 0.1 * rng.random((N, 128, 8, 4))
    a[o == 0] = 1
    a = 2.0 ** 30 * a * (rng.permutation(8) % 2 * 2.0 - 1.0)[:, None]
    u[:, :, ::16] = a.astype(np.float32).astype(BF)
    w = np.zeros((N, 128, 4, 128, 4), np.float32)
    i = np.arange(128)
    for b in range(4): w[:, i, b, i, b] = -1
    return {"x": (2.0 ** 30 * x * c).astype(np.float32).reshape(N, 128, 4 * C).astype(BF), "u": u.reshape(N, 128, 512), "v": d["v"], **lists(rng), **weights(rng, w.astype(BF))}
def setup_inputs_caps(rng):
    d = numbers_of(rng)
    u = d["u"].reshape(N, 128, 128, 4)
    u[:, :, ::16] = 0
    n, t = C // 8, T // 8
    back = {8: [[1], [6, 7]], 4: [[1, 2], [0, 2, 3]]}[N]
    size = rng.permutation(np.array([[t, t], [t, t], [t + 1, t - 1], [t - 1, t + 1], [n, 0], [0, n], [t, n - t], [n - t, t]]))
    a = np.zeros((N, 8, n, 8), int) + np.arange(8)
    for g in range(8):
        o = rng.permutation(n)
        i, j = int(size[g, 0]), int(size[g, 0] + size[g, 1])
        for r in back[0]: a[r, g, o[:i]] = np.arange(7, -1, -1)
        for r in back[1]: a[r, g, o[i:j]] = np.arange(7, -1, -1)
        for r in range(N): a[r, g, o[j:]] = np.array([7, 5, 6, 3, 4, 1, 2, 0] if r % 2 else [1, 0, 3, 2, 5, 4, 7, 6])
    return {"x": d["x"], "u": u.reshape(N, 128, 512), "v": d["v"], **lists(rng, a), **layers(rng)}
def setup_inputs_spread(rng):
    d = setup_inputs(rng)
    d["x"] = big(wide(rng, N, 128, 4 * C, cols=6))
    return d
def check_inputs(d):
    b = []
    for k in ("x", "u", "v"):
        a = np.abs(d[k].astype(np.float32))
        if not (np.isfinite(a).all() and ((a == 0) | (a >= 2.0 ** -30) & (a <= 2.0 ** 30)).all()): b.append("a value of " + k)
    none, least, most = [emit(mx_ref.quantize(np.full((128, 16), k, np.float32).astype(BF)))[1][0, 0] for k in (0.0, 2.0 ** -30, 2.0 ** 30)]
    for r in range(N):
        if (np.sort(gentries(d["p"][r]).reshape(8, -1, 8), axis=2).reshape(8, C) != np.arange(C)).any(): b.append("p: a block that doesn't hold its letters")
        if (np.sort(gentries(d["h"][r]), axis=1) != np.arange(C)).any(): b.append("h: a group that doesn't name every column once")
        if ((d["wc"][r] == 0x7F) | (d["wc"][r] == 0xFF)).any(): b.append("wc: a code that is no number")
        s = mx_ref.live(d["ws"][r])
        if ((s != none) & ((s < least) | (s > most))).any(): b.append("ws: a scale out of range")
    return b
def meet(a, b):
    a, b = a.reshape(8, -1, 8), np.argsort(b.reshape(8, -1, 8), axis=2)
    up = np.arange(8)[:, None] < np.arange(8)
    k = up & ((a[:, :, :, None] > a[:, :, None, :]) | (b[:, :, :, None] < b[:, :, None, :]))
    for i in range(8): k = k | (k[:, :, :, i:i + 1] & k[:, :, i:i + 1, :])
    return (np.sum(k, axis=2) + np.sum(up & ~k, axis=3)).reshape(8, C) + np.arange(C) // 8 * 8
def reference(x, u, v, p, h, wc, ws):
    qu = [mx_ref.quantize(u[r]) for r in range(N)]
    lay = [pk(wc[r], ws[r]) for r in range(N)]
    now = [x[r] for r in range(N)]
    word = [gentries(p[r]) for r in range(N)]
    home = [gentries(h[r]) for r in range(N)]
    for step in STEPS:
        for r in range(N):
            s = mx_ref.matmul(qu[r], mx_ref.quantize(now[r]))[::16] + np.float32(0.0)
            s = np.take_along_axis(s, np.take_along_axis(home[r], word[r], axis=1), axis=1).reshape(8, -1, 2)
            a = word[r].reshape(8, -1, 2)
            word[r] = np.where(s[:, :, :1] < s[:, :, 1:], a[:, :, ::-1], a).reshape(8, C)
        m = [None] * N
        for r in range(N):
            e = r ^ step
            if r < e:
                pos = meet(word[r], word[e])
                m[r] = m[e] = np.argsort(pos, axis=1)
                word[r], word[e] = np.take_along_axis(word[r], m[r], axis=1), np.take_along_axis(pos, word[e], axis=1)
        made, slot, sent = [], [], []
        for r in range(N):
            z = gcols(now[r], np.take_along_axis(home[r], word[r], axis=1))
            q = mx_ref.quantize(z)
            made.append(tile([mx_ref.matmul(pick(lay[r], np.arange(128 * b, 128 * b + 128)), q) * np.float32(0.03125) + z[:, b::4].astype(np.float32) for b in range(4)]))
            moved = m[r] != np.arange(C)
            o = np.argsort(~moved, axis=1, kind="stable")[:, :T]
            e = np.where(np.take_along_axis(moved, o, axis=1), o, -1)
            k = np.full((8, C + 1), -1)
            np.put_along_axis(k, np.where(e < 0, C, e), np.zeros((8, 1), int) + np.arange(T), axis=1)
            slot.append(k[:, :C])
            sent.append(mx_ref.quantize(gcols(made[r], e)))
        for r in range(N):
            came = gcols(decode(sent[r ^ step]).astype(BF), slot[r]).astype(np.float32)
            own = made[r].astype(np.float32)
            met = np.repeat(np.repeat(slot[r] >= 0, 16, axis=0), 4, axis=1)
            now[r] = np.where(met, (own + came) * np.float32(0.5), own).astype(BF)
    y, op = np.zeros((N, 128, C), np.float32), np.zeros((N, 8, C), np.float32)
    oc, osc = np.zeros((N, 128, 4 * C), np.uint8), np.zeros((N, 16, C), np.uint8)
    for r in range(N):
        q = mx_ref.quantize(now[r])
        y[r] = mx_ref.matmul(mx_ref.quantize(v[r]), q)
        op[r] = word[r]
        oc[r], osc[r] = emit(q)
    return {"y": y, "op": op, "oc": oc, "osc": osc}

@@ -1,0 +1,522 @@
+from concourse.mybir import dt, AluOpType as A, AxisListType, ActivationFunctionType as AF
+
+C, NT, STEPS = 512, 224, [1, 2, 3]
+YW = C + NT
+CODE = "float8_e4m3fn_x4"
+SCRATCH = {}
+POOL, _at = {}, [0]
+
+
+def _buf(name, n, dtype, where="sbuf"):
+    SCRATCH[name] = (where, [128, n], dtype)
+
+
+for _n, _w in [("x0", 2048), ("xa", 2048), ("xl", 2048), ("z", 2048), ("z32", 2048), ("yg", 4 * YW), ("ft", 4 * NT), ("f16", 4 * NT), ("ut", 512), ("vt", 512),
+               ("et", 2048), ("fl", 256), ("fsc", 256), ("sel2", 256), ("w", 512), ("b0", 128), ("lg", 128), ("d12", 256), ("pp", 128), ("x1", 208), ("o1", 208),
+               ("own", 208), ("wi", 256), ("cmp", 256), ("pos", 256), ("ne", 256), ("nw", 256), ("dtl", 256), ("kslow", 256), ("tfast", 256),
+               ("tslow", 256), ("rst8", 256), ("rneg8", 256), ("rst4", 128), ("ones", 256), ("sig", 128), ("sg1", 128), ("sg2", 128), ("nei", 256), ("rsc", 256),
+               ("wd", 32), ("w0", 32), ("r0", 32), ("df", 32), ("dd", 16), ("tt", 16), ("itab", 32)]:
+    _buf(_n, _w, "bfloat16")
+for _r in range(3):
+    _buf("snd%d" % _r, 32, "bfloat16"); _buf("lnd%d" % _r, 32, "bfloat16")
+    _buf("qf%d" % _r, NT, CODE); _buf("sf%d" % _r, NT, "uint8"); _buf("lq%d" % _r, NT, CODE); _buf("ls%d" % _r, NT, "uint8")
+for _n, _w in [("qx", 512), ("qz", 512), ("qw", 512), ("qe", 512), ("qu", 128), ("qu2", 128), ("qv", 128)]:
+    _buf(_n, _w, CODE); _buf("s" + _n[1:], _w, "uint8")
+for _n, _w in [("ssb", 512), ("bs", 256), ("iota", 512), ("selk", 512), ("erow", 1536), ("esc", NT), ("hrow", 512), ("hw", 512), ("hsc", 512), ("yo", 512),
+               ("pv", 16), ("s16", 48), ("rows", 208), ("oh", 208), ("r16", 208), ("vecs", 208), ("q8", 16), ("q32", 16), ("c2", 16), ("idm", 128),
+               ("t64", 64), ("u64", 64), ("mv", 32), ("cc", 32), ("h1", 32), ("h3", 32), ("h4", 32), ("tabn", 32), ("tabd", 32), ("mlt", 32), ("tr", 32),
+               ("base", 2), ("opf", 32), ("onef", 32), ("hf", 32), ("qk", 16)]:
+    _buf(_n, _w, "float32")
+for _n, _w in [("pi", 32), ("hi", 32), ("ia", 32), ("ib", 32), ("si", 8)]:
+    _buf(_n, _w, "int32")
+for _n, _w in [("il", 14), ("kl", 14), ("gl", 8), ("rkk", 16), ("rki", 16), ("posl", 16), ("mvl", 2), ("slow", 16), ("fast", 16), ("sgl", 8), ("rep", 32),
+               ("h0", 128), ("h1l", 128), ("hn", 32), ("hp", 32), ("zl", 32), ("al", 16), ("bl", 16), ("tot", 2), ("dst", 32), ("el", 14), ("xll", 32)]:
+    POOL[_n] = ("lists", _at[0], _w)
+    _at[0] += -(-_w // 16) * 16
+_buf("lists", _at[0], "uint16")
+_buf("ul", 8, "uint16")
+_buf("ps", 4096, "float32", "psum")
+SEMAPHORES = ["qv", "qs", "qt", "qg", "sent"] + ["d%d" % i for i in range(24)] + ["a%d" % i for i in range(9)]
+
+F = [1.25, 1.5, 2.0, 4.0, 16.0, 256.0, 2.0 ** 16, 2.0 ** 32]
+GI = [[0, 5, 4, 0, 0, 4, 0, 0, 6, 5, 4, 0, 6, 4, 0, 0], [0, 0, 3, 3, 3, 3, 3, 3, 2, 2, 2, 2, 2, 3, 0, 0], [1, 1, 1, 1, 1, 1, 1, 1, 0, 0, 0, 0, 0, 0, 1, 0]]
+GK0 = [0, 6, 5, 0, 0, 6, 0, 0, 7, 7, 7, 7, 7, 7, 0, 0]
+W7, B3, B2, B1, B0 = 0, 1, 2, 3, 4
+W6, W5, W4A, W4B = 129, 131, 133, 139
+W4, W3, W2, W1, W0 = 258, 270, 282, 398, 412
+LOC = [W0, W1, W2, W3, W4, W5, W6, W7]
+P1 = [W4A, W4B, W4B, W7, W6, W5, W4A, B3, W4B, W7, W6, W5, W4A, B2, W7, W7]
+P2 = [W7, W7, W6, W5, W4, W3, W2, B1, W7, W6, W5, W4, W3, W2, B0, W7]
+NONE = [0] * 16
+ROWS = GI + [NONE, GK0, NONE, NONE, P1, P2, LOC + LOC]
+NR = len(ROWS)
+LPLAN = [(w[0], int(w[1]), int(w[2])) for w in "q00 z00 z01 s10 s11 s02 s12 s03 s13 e00 q10 l00 a00 a10 a01 a11 a02 a12 a03 a13".split()]
+FPLAN = [("s", 0, 0, 14), ("s", 1, 0, 14), ("s", 2, 0, 14), ("v", 3, 0, 8), ("s", 3, 8, 14)]
+XPLAN = [("s", 0, 256, 0), ("s", 0, 256, 1), ("s", 0, 256, 2), ("v", 0, 256, 3), ("s", 256, 512, 0), ("s", 256, 512, 1), ("v", 256, 512, 3), ("q", 0, 256, "s"),
+         ("v", 256, 512, 2), ("q", 256, 512, "v")]
+
+
+def _cover(vals):
+    out = []
+    for v in sorted(set(vals) - {0}):
+        left = [i for i, x in enumerate(vals) if x == v]
+        while left:
+            best = [left[0]]
+            for s in range(1, len(vals)):
+                run = [left[0]]
+                while run[-1] + s in left:
+                    run.append(run[-1] + s)
+                if len(run) > len(best):
+                    best = run
+            out.append((v, best[0], best[-1] + 1, best[1] - best[0] if len(best) > 1 else 1))
+            left = [i for i in left if i not in best]
+    return out
+
+
+def rank_program(g, core, T, topo):
+    rank = T.rank_of(core)
+    if rank is None:
+        return
+    Q = {"v": g.vector, "s": g.scalar, "t": g.tensor, "g": g, "y": g.sync}
+    count = {"v": 0, "s": 0, "t": 0, "g": 0}
+    seen = {q: {} for q in Q}
+    total = {}
+    log = {}
+    nd = [0]
+
+    def V(name, a=0, b=None, s=1):
+        if name in POOL:
+            pool, at, n = POOL[name]
+            return (pool, at + a, at + (n if b is None else b), s)
+        return (name, a, SCRATCH[name][1][1] if b is None else b, s)
+
+    def I(win, off):
+        return ("ind", win, off)
+
+    def ap(v, cast=None):
+        if not isinstance(v, tuple):
+            return v
+        if v[0] == "ind":
+            return ap(v[1], cast).indirect(ap(v[2]))
+        a = T[v[0]][:, v[1]:v[2]:v[3]] if v[3] != 1 else T[v[0]][:, v[1]:v[2]]
+        return a.bitcast(cast) if cast is not None else a
+
+    def cols(v):
+        if v[0] == "ps":
+            return set(range(v[1] // 512, (v[2] - 1) // 512 + 1))
+        return set(range(v[1], v[2], v[3]))
+
+    def wait(q, tok):
+        if seen[q].get(tok[0], 0) < tok[1]:
+            Q[q].wait_ge(T.sem[tok[0]], tok[1])
+            seen[q][tok[0]] = tok[1]
+
+    def order(q, outs, ins, tok):
+        rd, wr = [], []
+        for v in ins:
+            if isinstance(v, tuple):
+                rd += [v[1], v[2]] if v[0] == "ind" else [v]
+        for v in outs:
+            if v[0] == "ind":
+                wr.append(v[1]); rd.append(v[2])
+            else:
+                wr.append(v)
+        need = {}
+        for vs, w in ((rd, False), (wr, True)):
+            for v in vs:
+                cs = cols(v)
+                for e in log.setdefault(v[0], []):
+                    same = e[2][0] == "q" + q
+                    if (e[1] or (w and not same) or (v[0] == "ps" and not same)) and cs & e[0]:
+                        need[e[2][0]] = max(need.get(e[2][0], 0), e[2][1])
+        for s in sorted(need):
+            wait(q, (s, need[s]))
+        for v in wr:
+            cs = cols(v)
+            log[v[0]] = [e for e in log[v[0]] if not e[0] <= cs] + [(cs, True, tok)]
+        for v in rd:
+            log[v[0]].append((cols(v), False, tok))
+
+    def call(q, outs, ins, make):
+        count[q] += 1
+        tok = ("q" + q, count[q])
+        order(q, outs, ins, tok)
+        make().then_inc(T.sem["q" + q], 1)
+        total["q" + q] = count[q]
+
+    def dma(q, out, in_, outs, ins):
+        tok = ("d%d" % nd[0], 16)
+        nd[0] += 1
+        order(q, outs, ins, tok)
+        Q[q].dma_start(out, in_).then_inc(T.sem[tok[0]], 16)
+        total[tok[0]] = 16
+
+    def send(peer, dst, src, sem, cast=None):
+        rid, pid, _e = topo.addr(peer)
+        total["sent"] = total.get("sent", 0) + len(topo.engines(core, peer))
+        order("g", [], [src], ("sent", 0))
+        g.remote_dma(ap(dst, cast), ap(src, cast), T.sem[sem], T.sem.sent, pid, rid, topo.mask(core, peer))
+        total[sem] = len(topo.engines(peer, core))
+        log[dst[0]] = [(cols(dst), True, (sem, total[sem]))]
+
+    def cp(o, i): call("v", [o], [i], lambda: g.vector.tensor_copy(ap(o), ap(i)))
+    def tt(o, a, b, op): call("v", [o], [a, b], lambda: g.vector.tensor_tensor(ap(o), ap(a), ap(b), op))
+    def ts(o, a, s1, op, s2=None, op1=None):
+        if op1 is None:
+            call("v", [o], [a, s1], lambda: g.vector.tensor_scalar(ap(o), ap(a), ap(s1), None, op))
+        else:
+            call("v", [o], [a, s1, s2], lambda: g.vector.tensor_scalar(ap(o), ap(a), ap(s1), ap(s2), op, op1))
+    def scan(o, a, b, op0, op1): call("v", [o], [a, b], lambda: g.vector.tensor_tensor_scan(ap(o), ap(a), ap(b), 0.0, op0, op1))
+    def ms(o, c): call("v", [o], [], lambda: g.vector.memset(ap(o), c))
+    def act(o, i, c=1.0): call("s", [o], [i], lambda: g.scalar.activation(ap(o), ap(i), AF.Copy, scale=float(c)))
+    def move(q, o, i, c=1.0):
+        if q == "s":
+            act(o, i, c)
+        elif c == 1.0:
+            cp(o, i)
+        else:
+            ts(o, i, float(c), A.mult)
+    def quant(q, t, a, b): call("v", [V("q" + q, a, b), V("s" + q, a, b)], [t], lambda: g.vector.quantize_mx(ap(V("q" + q, a, b)), ap(V("s" + q, a, b)), ap(t)))
+    def mm(bank, l, r):
+        o = V("ps", 512 * bank, 512 * bank + r[0][2] - r[0][1])
+        call("t", [o], list(l) + list(r), lambda: g.tensor.matmul_mx(ap(o), ap(l[0]), ap(l[1]), ap(r[0]), ap(r[1]), True, True))
+        return o
+    def mx(q, a, b): return (V("q" + q, a, b), V("s" + q, a, b))
+    def iota(o, pat, base, cm):
+        small = SCRATCH[o[0]][2] != "int32"
+        call("g", [o], [], lambda: g.iota(ap(o), pat, base, cm, allow_small_or_imprecise_dtypes=True) if small else g.iota(ap(o), pat, base, cm))
+    def trans(o, i): call("v", [o], [i], lambda: g.vector.transpose(ap(o), ap(i)))
+    def col(name, j): return V(name, j, j + 1)
+    def one(o, c): act(o, V("ones", 0, len(range(o[1], o[2], o[3]))), c)
+
+    roles = [rank < rank ^ s for s in STEPS]
+    dma("s", ap(V("pi")), T.p[:], [V("pi")], [])
+    dma("y", ap(V("ut")), T.u[:], [V("ut")], [])
+    dma("s", ap(V("hi")), T.h[:], [V("hi")], [])
+    for k in range(2):
+        dma("y", ap(V("x0", 1024 * k, 1024 * k + 1024)), T.x[:, 1024 * k:1024 * k + 1024], [V("x0", 1024 * k, 1024 * k + 1024)], [])
+    dma("y", ap(V("qw"), dt.uint8), T.wc[:], [V("qw")], [V("x0")])
+    dma("y", ap(V("sw")), T.ws[:], [V("sw")], [])
+    dma("y", ap(V("vt")), T.v[:], [V("vt")], [])
+
+    ms(V("ones"), 1.0)
+    ms(V("rows"), 0.0)
+    iota(V("si", 0, 2), [[0, 2]], 0, 1)
+    iota(V("s16", 0, 16), [[1, 16]], 0, 0)
+    iota(V("ia", 0, 8), [[16, 8]], 0, 0)
+    iota(V("q8"), [[8, 4], [0, 4]], 0, 0)
+    if not roles[0]:
+        iota(V("tslow"), [[8, 4], [1, 8], [0, 8]], 0, 0)
+    iota(V("c2"), [[2, 16]], 0, 0)
+    iota(V("rows", 48, 56), [[-2, 2], [8, 4]], 2, 0)
+    iota(V("rows", 82, 94), [[0, 2], [-1, 6]], 8, 0)
+    iota(V("rows", 97, 111), [[0, 2], [-1, 7]], 7, 0)
+    iota(V("r16", 0, 16 * NR), [[0, NR], [1, 16]], 0, 0)
+    iota(V("qk"), [[0, 8], [64, 2]], 0, 0)
+    if roles[0]:
+        iota(V("kslow"), [[0, 4], [1, 8], [0, 8]], 0, 0)
+    else:
+        iota(V("tfast"), [[8, 4], [0, 8], [1, 8]], 0, 0)
+    iota(V("itab"), [[0, 4], [1, 8]], 0, 0)
+    iota(V("iota"), [[1, 512]], 0, 0)
+    ms(V("onef"), 1.0)
+    ms(V("w"), 0.0); ms(V("b0"), 0.0); ms(V("d12"), 1.0)
+    ts(V("si", 2, 3), col("si", 0), 15, A.bitwise_and)
+    ts(V("si", 3, 4), col("si", 0), 7, A.bitwise_and)
+    ts(V("si", 4, 5), col("si", 0), 3, A.logical_shift_right, 1, A.bitwise_and)
+    ts(V("si", 5, 6), col("si", 0), 4, A.logical_shift_right, 1, A.bitwise_and)
+    ts(V("si", 6, 7), col("si", 0), 3, A.bitwise_and)
+    cp(V("ul"), V("ia", 0, 8))
+    cp(col("pv", 0), col("si", 2)); cp(V("pv", 2, 4), V("si", 3, 5)); cp(col("pv", 5), col("si", 5))
+    ts(col("pv", 1), col("si", 2), 1.0, A.add)
+    ts(col("pv", 4), col("si", 5), -1.0, A.mult, 1.0, A.add)
+    ts(col("pv", 6), col("si", 2), 32.0, A.mult)
+    ts(col("pv", 8), col("si", 2), 15.0, A.is_lt, 2.0, A.mult)
+    ts(col("pv", 11), col("si", 6), 16.0, A.mult, 15.0, A.add)
+    ts(V("s16", 16, 32), V("s16", 0, 16), col("pv", 0), A.is_equal, -4096.0, A.mult)
+    ts(V("s16", 32, 48), V("s16", 0, 16), col("pv", 1), A.is_equal, 1024.0, A.mult)
+    ts(V("rep"), V("onef"), col("pv", 0), A.mult)
+    tt(V("s16", 16, 32), V("s16", 16, 32), V("s16", 32, 48), A.add)
+    ts(V("fast"), V("q8"), col("pv", 2), A.add)
+    ms(V("rst4"), 1.0)
+    ts(V("sgl"), V("q8", 0, 16, 2), 8.0, A.mult, col("pv", 11), A.add)
+    ms(V("rst4", 0, 128, 4), 0.0)
+    for v, a, b, s in _cover([x for r in ROWS for x in r]):
+        one(V("rows", a, b, s), v)
+    one(V("rows", 82, 94, 6), 4.0)
+    act(V("sel2"), I(V("s16", 16, 32), V("rep", 0, 16)), 2.0 ** -9)
+
+    for v in range(2):
+        for e in range(2):
+            ts(V("t64", 32 * v + 16 * e, 32 * v + 16 * e + 16), V("pi", v, 32, 2), col("pv", 4 + e), A.mult)
+    trans(V("u64"), V("t64"))
+    for v in range(2):
+        tt(V("opf", 16 * v, 16 * v + 16), V("u64", 32 * v, 32 * v + 16), V("u64", 32 * v + 16, 32 * v + 32), A.add)
+    quant("u", V("ut"), 0, 128)
+    ts(V("wd"), V("opf"), col("pv", 6), A.subtract)
+    cp(V("al"), V("opf", 0, 32, 2)); cp(V("bl"), V("opf", 1, 32, 2))
+    call("v", [V("qu2")], [I(V("qu"), V("ul"))], lambda: g.vector.tensor_copy(ap(V("qu2"), dt.uint32), ap(I(V("qu"), V("ul")), dt.uint32)))
+    call("s", [V("su2")], [I(V("su"), V("ul"))], lambda: g.scalar.activation(ap(V("su2")), ap(I(V("su"), V("ul"))), AF.Copy))
+    cp(V("hn"), V("hi"))
+
+    def fixed():
+        one(V("w", W7, 128, 32), 1.0)
+        for at, i in ((B3, 3), (B2, 2), (B1, 1), (B0, 0)):
+            one(V("w", at, 128, 32), F[i] / F[7])
+        for at, i in ((1, 6), (3, 5), (5, 4), (9, 6), (11, 4)):
+            one(V("b0", at, 128, 32), F[i]); one(V("b0", 16 + at, 128, 32), F[i] / F[7])
+        for at, c in ((0, 0.0), (2, 0.0), (7, F[3]), (13, F[2]), (14, 0.0), (64, 0.0), (65, 0.0), (71, F[1]), (78, F[0]), (79, 0.0)):
+            one(V("d12", at, 64 * (at // 64) + 64, 16), c)
+
+    def tables():
+        vec = lambda n: col("vecs", 16 * n + 15)
+        n = 16 * NR
+        ts(V("oh", 0, n), V("r16", 0, n), col("pv", 0), A.is_equal)
+        ts(V("r16", 0, n), V("r16", 0, n), 0.0, A.is_gt)
+        tt(V("oh", 0, n), V("oh", 0, n), V("rows", 0, n), A.mult)
+        ts(V("slow"), V("c2"), col("pv", 3), A.add)
+        scan(V("vecs", 0, n), V("r16", 0, n), V("oh", 0, n), A.mult, A.add)
+        ms(V("rst8"), 1.0)
+        for n in range(3):
+            ts(V("il", 4 * n, 4 * n + 4), V("q8", 0, 16, 4), vec(n), A.add)
+            ts(V("kl", 4 * n, 4 * n + 4), V("q8", 0, 16, 4), vec(4 + n), A.add)
+        cp(V("il", 12, 13), vec(3))
+        ts(V("kl", 12, 13), vec(3), 1.0, A.add)
+        ms(V("rst8", 0, 256, 8), 0.0)
+
+    def rank_tables():
+        vec = lambda n: col("vecs", 16 * n + 15)
+        ts(col("pv", 9), col("si", 4), 32.0, A.mult)
+        ts(col("pv", 10), col("si", 3), 32.0, A.mult, 7.0, A.add)
+        ts(V("q32"), V("q8"), 4.0, A.mult)
+        ts(col("pv", 7), col("si", 2), 15.0, A.is_lt, 1024.0, A.mult)
+        ts(V("qk"), V("qk"), col("pv", 9), A.add)
+        ts(col("pv", 12), col("si", 4), 8.0, A.mult, col("pv", 10), A.add)
+        ts(V("posl"), V("q8"), col("pv", 10), A.add)
+        for n in range(2):
+            ts(V("gl", 4 * n, 4 * n + 4), V("q32", 0, 16, 4), vec(7 + n), A.add)
+        if not all(roles):
+            ts(V("rneg8"), V("rst8"), 128.0, A.mult, -128.0, A.add)
+        ts(V("rkk"), V("qk"), vec(9), A.add)
+        ts(V("mvl"), V("c2", 0, 16, 8), col("pv", 12), A.add)
+        for i in range(8):
+            ts(V("rki", 2 * i, 2 * i + 2), V("qk", 0, 2), float(LOC[i]), A.add)
+
+    def moved_tables():
+        ms(V("mlt", 0, 16), 0.0)
+        ts(V("mlt", 16, 32), V("s16", 0, 16), col("pv", 0), A.is_lt)
+        ms(V("erow", 0, NT), 0.0)
+        ts(V("tabd"), V("iota", 0, 32), 512.0, A.add, col("pv", 6), A.add)
+
+    def late():
+        iota(V("idm"), [[1, 128]], 0, -1)
+        ts(V("ia"), V("hi"), 31, A.bitwise_and)
+        ts(V("ib"), V("hi"), 5, A.logical_shift_right)
+        ts(V("tabn"), V("iota", 0, 32), 16.0, A.mult, col("pv", 0), A.add)
+        ts(V("hf"), V("ia"), 16.0, A.mult)
+        ms(V("et"), 0.0)
+        tt(V("hf"), V("hf"), V("ib"), A.add)
+        for b in range(4):
+            ts(V("et", 513 * b, 512 * b + 512, 4), V("idm"), 0.0, A.is_equal, 16.0, A.mult)
+            if b == 0:
+                cp(V("hp"), V("hf"))
+        quant("e", V("et"), 0, 512)
+        act(V("hrow"), I(V("iota"), V("hp")))
+        if roles[0] and not all(roles):
+            iota(V("tslow"), [[8, 4], [1, 8], [0, 8]], 0, 0)
+            iota(V("tfast"), [[8, 4], [0, 8], [1, 8]], 0, 0)
+        if not roles[0] and any(roles):
+            iota(V("kslow"), [[0, 4], [1, 8], [0, 8]], 0, 0)
+
+    def prepare(left):
+        tt(V("dd"), V("wd", 1, 32, 2), V("wd", 0, 32, 2), A.subtract)
+        if not left:
+            tt(V("nei"), I(V("wd"), V("fast")), V("tslow"), A.not_equal)
+        ts(V("tt"), V("dd"), col("pv", 8), A.mult)
+        if not left:
+            tt(V("sig"), V("nei", 0, 256, 2), V("nei", 1, 256, 2), A.subtract)
+            scan(V("rsc"), V("nei"), V("ones"), A.mult, A.add)
+        tt(V("w0", 0, 32, 2), V("wd", 0, 32, 2), V("tt"), A.subtract)
+        if not left:
+            scan(V("sg2"), V("rst4"), V("sig"), A.mult, A.add)
+        tt(V("w0", 1, 32, 2), V("wd", 1, 32, 2), V("tt"), A.add)
+        if not left:
+            ts(V("r0"), V("sg2", 3, 128, 4), col("pv", 8), A.mult)
+            tt(V("r0"), V("rsc", 7, 256, 8), V("r0"), A.subtract)
+
+    prepare(roles[0])
+    for k in range(2):
+        quant("x", V("x0", 1024 * k, 1024 * k + 1024), 256 * k, 256 * k + 256)
+        act(V("ssb", 256 * k, 256 * k + 256), mm(k, mx("u2", 0, 128), mx("x", 256 * k, 256 * k + 256)))
+    for b in range(4):
+        ts(V("h0", 32 * b, 32 * b + 32), V("hi"), 4.0, A.mult, float(b), A.add)
+    xcur = "x0"
+    for r, step in enumerate(STEPS):
+        peer = T.cores[rank ^ step]
+        left = roles[r]
+        last = r == len(STEPS) - 1
+        snd, lnd = "snd%d" % r, V("lnd%d" % r)
+        src = "ssb"
+        if r == 0:
+            src = "hsc"
+            act(V(src, 0, 256), I(V("ssb"), V("hn", 0, 16)))
+            cp(V(src, 256, 512), I(V("ssb"), V("hn", 16, 32)))
+        act(V("bs", 128, 256), I(V(src), V("bl", 8, 16)))
+        cp(V("bs", 0, 128), I(V(src), V("bl", 0, 8)))
+        for k in range(2):
+            tt(V("fl", 128 * k, 128 * k + 128), I(V(src), V("al", 8 * k, 8 * k + 8)), V("bs", 128 * k, 128 * k + 128), A.is_lt)
+        scan(V("fsc"), V("sel2"), V("fl"), A.add, A.max)
+        word = snd if left else "df"
+        if not left:
+            tt(V("sg1"), I(V("fsc"), V("sgl")), V("sig"), A.mult)
+        tt(V("tt"), V("fsc", 15, 256, 16), V("dd"), A.mult)
+        if not left:
+            scan(V("sg2"), V("rst4"), V("sg1"), A.mult, A.add)
+        tt(V(word, 0, 32, 2), V("w0", 0, 32, 2), V("tt"), A.add)
+        if not left:
+            tt(V(snd), V("r0"), V("sg2", 3, 128, 4), A.add)
+        tt(V(word, 1, 32, 2), V("w0", 1, 32, 2), V("tt"), A.subtract)
+        send(peer, lnd, V(snd), "a%d" % (3 * r))
+        if r == 0:
+            fixed()
+            tables()
+        cp(V("o1"), I(V(snd), V("il", 0, 13)))
+        if left:
+            tt(V("df", 0, 31), V(snd, 0, 31), V(snd, 1, 32), A.subtract)
+        tt(V("own"), I(V(snd), V("kl", 0, 13)), V("o1"), A.is_le)
+        if left:
+            cp(V("df", 7, 32, 8), V(snd, 7, 32, 8))
+        else:
+            tt(V("dtl"), I(V(word), V("slow")), V("tfast"), A.is_equal)
+        ts(V("own"), V("own"), 64.0, A.mult)
+        if left:
+            cp(V("dtl"), I(V("df"), V("fast")))
+        else:
+            for q in range(4):
+                ts(V("dtl", 64 * q, 64 * q + 64), V("dtl", 64 * q, 64 * q + 64), 64.0, A.mult, 8.0 * q - 64.0, A.add)
+        hl = "h0" if r == 0 else "h1l"
+        for b in range(4):
+            act(V("xl", 512 * b, 512 * b + 512), I(V(xcur), V(hl, 32 * b, 32 * b + 32)))
+        if r == 0:
+            rank_tables()
+            moved_tables()
+        tt(V("x1", 0, 64), I(lnd, V("il", 0, 4)), V("own", 0, 64), A.add)
+        tt(V("x1", 64, 208), I(lnd, V("il", 4, 13)), V("own", 64, 208), A.add)
+        tt(V("b0", 0, 128, 2), I(lnd, V("kl", 0, 4)), V("x1", 0, 64), A.is_le)
+        tt(V("lg", 0, 64), I(lnd, V("kl", 4, 8)), V("x1", 64, 128), A.is_le)
+        scan(V("w", 128, 240), V("b0", 0, 112), V("b0", 16, 128), A.mult, A.max)
+        tt(V("d12", 8, 256, 16), I(lnd, V("kl", 12, 13)), V("x1", 192, 208), A.is_le)
+        tt(V("pp", 0, 64), I(V("w", 0, 256), V("gl", 0, 4)), V("lg", 0, 64), A.mult)
+        tt(V("lg", 64, 128), I(lnd, V("kl", 8, 12)), V("x1", 128, 192), A.is_le)
+        scan(V("w", 256, 384, 2), V("d12", 0, 64), V("pp", 0, 64), A.mult, A.max)
+        act(V("wi", 64, 256), I(V("w", 0, 384), V("rki", 4, 16)))
+        tt(V("pp", 64, 128), I(V("w", 0, 384), V("gl", 4, 8)), V("lg", 64, 128), A.mult)
+        scan(V("w", 384, 512, 2), V("d12", 64, 128), V("pp", 64, 128), A.mult, A.max)
+        cp(V("wi", 0, 64), I(V("w"), V("rki", 0, 4)))
+        tt(V("cmp", 64, 256), I(V("w"), V("rkk", 4, 16)), V("wi", 64, 256), A.is_gt)
+        tt(V("cmp", 0, 64), I(V("w"), V("rkk", 0, 4)), V("wi", 0, 64), A.is_gt)
+        if r == 0:
+            act(V("selk"), I(V("s16", 16, 32), V("rep")))
+        scan(V("pos"), V("rst8"), V("cmp"), A.mult, A.add)
+        if left:
+            tt(V("ne"), I(V("pos"), V("posl")), V("kslow"), A.not_equal)
+        else:
+            tt(V("ne"), I(V("pos"), V("posl")), V("dtl"), A.add)
+        tt(V("mv"), I(V("pos"), V("mvl")), V("itab"), A.not_equal)
+        if left:
+            scan(V("nw"), V("ne"), V("dtl"), A.mult, A.add)
+        else:
+            scan(V("nw"), V("rneg8"), V("ne"), A.add, A.max)
+        scan(V("cc"), V("onef"), V("mv"), A.mult, A.add)
+        ts(V("zl"), V("nw", 7, 256, 8), col("pv", 6), A.add)
+
+        def gather_z(q, k, b):
+            move(q, V("z", 1024 * k + b, 1024 * k + 1024, 4), I(V("xl", 512 * b, 512 * b + 512), V("zl", 16 * k, 16 * k + 16)))
+
+        for k in range(2):
+            for b in range(4):
+                if ("g", k, b) not in LPLAN:
+                    gather_z("s", k, b)
+        cp(V("tot"), V("cc", 30, 32))
+        ts(V("h1"), V("mv"), -2048.0, A.mult, 2047.0, A.add)
+        tt(V("tr"), I(V("iota", 0, 64), V("tot")), V("mlt"), A.mult)
+        tt(V("h1"), V("h1"), V("cc"), A.add)
+        call("v", [col("base", 0)], [V("tr")], lambda: g.vector.tensor_reduce(ap(col("base", 0)), ap(V("tr")), AxisListType.X, A.add))
+        tt(V("h1"), V("h1"), V("tabd"), A.min)
+        cp(V("wd"), V("nw", 7, 256, 8))
+        ts(V("dst"), V("h1"), col("base", 0), A.add)
+        cp(I(V("erow"), V("dst")), V("iota"))
+        outs = {}
+        for what, k, b in LPLAN:
+            piece = V("z32", 512 * b + 256 * k, 512 * b + 256 * k + 256)
+            if what == "g":
+                gather_z("v", k, b)
+            elif what == "q":
+                quant("z", V("z", 1024 * k, 1024 * k + 1024), 256 * k, 256 * k + 256)
+                outs[k] = [mm(4 * k + n, mx("w", 128 * n, 128 * n + 128), mx("z", 256 * k, 256 * k + 256)) for n in range(4)]
+            elif what in "zs":
+                move("v" if what == "z" else "s", piece, V("z", 1024 * k + b, 1024 * k + 1024, 4), 32.0)
+            elif what == "a":
+                tt(V("yg", YW * b + 256 * k, YW * b + 256 * k + 256), outs[k][b], piece, A.add)
+            elif what == "e":
+                scan(V("esc"), V("selk", 0, NT), V("erow", 0, NT), A.add, A.max)
+            else:
+                ts(V("el"), V("esc", 15, NT, 16), col("pv", 7), A.subtract)
+        for q, b, c0, c1 in FPLAN:
+            move(q, V("ft", 64 * c0 + b, 64 * c1, 4), I(V("yg", YW * b, YW * b + C), V("el", c0, c1)), 2.0 ** -5)
+        quant("f%d" % r, V("ft"), 0, NT)
+        send(peer, V("lq%d" % r), V("qf%d" % r), "a%d" % (3 * r + 1), dt.uint8)
+        send(peer, V("ls%d" % r), V("sf%d" % r), "a%d" % (3 * r + 2))
+        if r == 0:
+            late()
+        ts(V("h3"), V("h1"), col("base", 0), A.add, float(NT), A.is_lt)
+        tt(V("h4"), V("h1"), V("tabn"), A.subtract)
+        ts(V("f16"), V("ft"), 16.0, A.mult)
+        ts(V("h4"), V("h4"), 512.0, A.add, col("base", 0), A.add)
+        tt(V("h4"), V("h4"), V("h3"), A.mult)
+        tt(V("h4"), V("h4"), V("tabn"), A.add)
+        if not last:
+            cp(V("xll"), V("h4"))
+            act(V("hw"), I(V("hrow"), V("zl")))
+            prepare(roles[r + 1])
+            scan(V("hsc"), V("selk"), V("hw"), A.add, A.max)
+            if r == 0:
+                for b in range(4):
+                    ts(V("h1l", 32 * b, 32 * b + 32), V("hf"), 4.0, A.mult, float(b), A.add)
+            else:
+                quant("v", V("vt"), 0, 128)
+            ts(V("al"), V("hsc", 15, 512, 32), col("pv", 7), A.subtract)
+            ts(V("bl"), V("hsc", 31, 512, 32), col("pv", 7), A.subtract)
+        else:
+            for v in range(2):
+                for e in range(2):
+                    ts(V("t64", 32 * v + 16 * e, 32 * v + 16 * e + 16), V("h4", 16 * v, 16 * v + 16), col("pv", 4 + e), A.mult)
+            trans(V("u64"), V("t64"))
+            for v in range(2):
+                tt(V("h3", v, 32, 2), V("u64", 32 * v, 32 * v + 16), V("u64", 32 * v + 16, 32 * v + 32), A.add)
+            cp(V("xll"), V("h3"))
+            ts(V("opf"), V("wd"), col("pv", 6), A.add)
+            dma("y", T.op[:], ap(V("opf")), [], [V("opf")])
+        for b in range(4):
+            o = mm(4 + b, mx("e", 128 * b, 128 * b + 128), (V("lq%d" % r), V("ls%d" % r)))
+            tt(V("yg", YW * b + C, YW * b + YW), o, V("f16", b, 4 * NT, 4), A.add)
+        xcur = "xa"
+        bank, after = 0, []
+        for q, a, e, b in XPLAN:
+            if q != "q":
+                move(q, V(xcur, 4 * a + b, 4 * e, 4), I(V("yg", YW * b, YW * b + YW), V("xll", a // 16, e // 16)), 2.0 ** -5)
+                continue
+            quant("x", V(xcur, 4 * a, 4 * e), a, e)
+            if last:
+                dma("y", T.oc[:, 4 * a:4 * e], ap(V("qx", a, e), dt.uint8), [], [V("qx", a, e)])
+            after.append((a, e, b, mm(bank, mx("v" if last else "u2", 0, 128), mx("x", a, e))))
+            bank += 1
+        for a, e, q, o in after:
+            move(q, V("yo" if last else "ssb", a, e), o)
+            if last:
+                dma("s", T.y[:, a:e], ap(V("yo", a, e)), [], [V("yo", a, e)])
+
+    for k in range(4):
+        dma("y", T.osc[4 * k:4 * k + 4, :], T.sx[32 * k:32 * k + 4, :], [], [V("sx")])
+    for s in sorted(total):
+        wait("g", (s, total[s]))

@@ -12,10 +12,10 @@ def _buf(name, n, dtype, where="sbuf"):
 
 
 for _n, _w in [("x0", 2048), ("xa", 2048), ("xl", 2048), ("z", 2048), ("z32", 2048), ("yg", 4 * YW), ("ft", 4 * NT), ("f16", 4 * NT), ("ut", 512), ("vt", 512),
-               ("et", 2048), ("fl", 256), ("fsc", 256), ("sel2", 256), ("w", 512), ("b0", 128), ("lg", 128), ("d12", 256), ("pp", 128), ("x1", 208), ("o1", 208),
-               ("own", 208), ("wi", 256), ("cmp", 256), ("pos", 256), ("ne", 256), ("nw", 256), ("dtl", 256), ("kslow", 256), ("tfast", 256),
+               ("et", 2048), ("six", 512), ("fl", 256), ("fsc", 256), ("sel2", 256), ("w", 512), ("b0", 128), ("lg", 128), ("d12", 256), ("pp", 128), ("x1", 208),
+               ("o1", 208), ("own", 208), ("wi", 256), ("cmp", 256), ("pos", 256), ("ne", 256), ("nw", 256), ("dtl", 256), ("kslow", 256), ("tfast", 256),
                ("tslow", 256), ("rst8", 256), ("rneg8", 256), ("rst4", 128), ("ones", 256), ("sig", 128), ("sg1", 128), ("sg2", 128), ("nei", 256), ("rsc", 256),
-               ("wd", 32), ("w0", 32), ("r0", 32), ("df", 32), ("dd", 16), ("tt", 16), ("itab", 32)]:
+               ("wd", 32), ("w0", 32), ("r0", 32), ("df", 32), ("dd", 32), ("v0", 32), ("lv0", 32), ("lv1", 32), ("tt", 16), ("itab", 32)]:
     _buf(_n, _w, "bfloat16")
 for _r in range(3):
     _buf("snd%d" % _r, 32, "bfloat16"); _buf("lnd%d" % _r, 32, "bfloat16")
@@ -23,20 +23,20 @@ for _r in range(3):
 for _n, _w in [("qx", 512), ("qz", 512), ("qw", 512), ("qe", 512), ("qu", 128), ("qu2", 128), ("qv", 128)]:
     _buf(_n, _w, CODE); _buf("s" + _n[1:], _w, "uint8")
 for _n, _w in [("ssb", 512), ("bs", 256), ("iota", 512), ("selk", 512), ("erow", 1536), ("esc", NT), ("hrow", 512), ("hw", 512), ("hsc", 512), ("yo", 512),
-               ("pv", 16), ("s16", 48), ("rows", 208), ("oh", 208), ("r16", 208), ("vecs", 208), ("q8", 16), ("q32", 16), ("c2", 16), ("idm", 128),
+               ("pv", 16), ("s16", 48), ("rows", 160), ("stg", 128), ("vecs", 160), ("q8", 16), ("q32", 16), ("c2", 16),
                ("t64", 64), ("u64", 64), ("mv", 32), ("cc", 32), ("h1", 32), ("h3", 32), ("h4", 32), ("tabn", 32), ("tabd", 32), ("mlt", 32), ("tr", 32),
                ("base", 2), ("opf", 32), ("onef", 32), ("hf", 32), ("qk", 16)]:
     _buf(_n, _w, "float32")
 for _n, _w in [("pi", 32), ("hi", 32), ("ia", 32), ("ib", 32), ("si", 8)]:
     _buf(_n, _w, "int32")
-for _n, _w in [("il", 14), ("kl", 14), ("gl", 8), ("rkk", 16), ("rki", 16), ("posl", 16), ("mvl", 2), ("slow", 16), ("fast", 16), ("sgl", 8), ("rep", 32),
+for _n, _w in [("il", 14), ("kl", 14), ("slow", 16), ("gl", 8), ("rkk", 16), ("rki", 16), ("posl", 16), ("mvl", 2), ("fast", 16), ("sgl", 8), ("rep", 32),
                ("h0", 128), ("h1l", 128), ("hn", 32), ("hp", 32), ("zl", 32), ("al", 16), ("bl", 16), ("tot", 2), ("dst", 32), ("el", 14), ("xll", 32)]:
     POOL[_n] = ("lists", _at[0], _w)
     _at[0] += -(-_w // 16) * 16
 _buf("lists", _at[0], "uint16")
 _buf("ul", 8, "uint16")
 _buf("ps", 4096, "float32", "psum")
-SEMAPHORES = ["qv", "qs", "qt", "qg", "sent"] + ["d%d" % i for i in range(24)] + ["a%d" % i for i in range(9)]
+SEMAPHORES = ["qv", "qs", "qt", "qg", "sent"] + ["d%d" % i for i in range(24)] + ["a%d" % i for i in range(10)]
 
 F = [1.25, 1.5, 2.0, 4.0, 16.0, 256.0, 2.0 ** 16, 2.0 ** 32]
 GI = [[0, 5, 4, 0, 0, 4, 0, 0, 6, 5, 4, 0, 6, 4, 0, 0], [0, 0, 3, 3, 3, 3, 3, 3, 2, 2, 2, 2, 2, 3, 0, 0], [1, 1, 1, 1, 1, 1, 1, 1, 0, 0, 0, 0, 0, 0, 1, 0]]
@@ -49,11 +49,10 @@ P1 = [W4A, W4B, W4B, W7, W6, W5, W4A, B3, W4B, W7, W6, W5, W4A, B2, W7, W7]
 P2 = [W7, W7, W6, W5, W4, W3, W2, B1, W7, W6, W5, W4, W3, W2, B0, W7]
 NONE = [0] * 16
 ROWS = GI + [NONE, GK0, NONE, NONE, P1, P2, LOC + LOC]
-NR = len(ROWS)
-LPLAN = [(w[0], int(w[1]), int(w[2])) for w in "q00 z00 z01 s10 s11 s02 s12 s03 s13 e00 q10 l00 a00 a10 a01 a11 a02 a12 a03 a13".split()]
+LPLAN = [(w[0], int(w[1]), int(w[2])) for w in "q00 z00 z01 z02 s10 s11 s12 s03 s13 e00 a00 q10 l00 a01 a10 a11 a02 a12 a03 a13".split()]
 FPLAN = [("s", 0, 0, 14), ("s", 1, 0, 14), ("s", 2, 0, 14), ("v", 3, 0, 8), ("s", 3, 8, 14)]
-XPLAN = [("s", 0, 256, 0), ("s", 0, 256, 1), ("s", 0, 256, 2), ("v", 0, 256, 3), ("s", 256, 512, 0), ("s", 256, 512, 1), ("v", 256, 512, 3), ("q", 0, 256, "s"),
-         ("v", 256, 512, 2), ("q", 256, 512, "v")]
+XPLAN = [("s", 0, 288, 0), ("s", 0, 288, 1), ("s", 0, 288, 2), ("v", 0, 288, 3), ("s", 288, 512, 0), ("s", 288, 512, 1), ("v", 288, 512, 3), ("q", 0, 288, "s"),
+         ("v", 288, 512, 2), ("q", 288, 512, "v")]
 
 
 def _cover(vals):
@@ -89,6 +88,9 @@ def rank_program(g, core, T, topo):
             pool, at, n = POOL[name]
             return (pool, at + a, at + (n if b is None else b), s)
         return (name, a, SCRATCH[name][1][1] if b is None else b, s)
+
+    def S(name, a=0, b=None, s=1):
+        return ("stg",) + V(name, a, b, s)[1:]
 
     def I(win, off):
         return ("ind", win, off)
@@ -126,8 +128,7 @@ def rank_program(g, core, T, topo):
             for v in vs:
                 cs = cols(v)
                 for e in log.setdefault(v[0], []):
-                    same = e[2][0] == "q" + q
-                    if (e[1] or (w and not same) or (v[0] == "ps" and not same)) and cs & e[0]:
+                    if (e[1] or w or (v[0] == "ps" and e[2][0] != "q" + q)) and cs & e[0]:
                         need[e[2][0]] = max(need.get(e[2][0], 0), e[2][1])
         for s in sorted(need):
             wait(q, (s, need[s]))
@@ -169,6 +170,7 @@ def rank_program(g, core, T, topo):
     def scan(o, a, b, op0, op1): call("v", [o], [a, b], lambda: g.vector.tensor_tensor_scan(ap(o), ap(a), ap(b), 0.0, op0, op1))
     def ms(o, c): call("v", [o], [], lambda: g.vector.memset(ap(o), c))
     def act(o, i, c=1.0): call("s", [o], [i], lambda: g.scalar.activation(ap(o), ap(i), AF.Copy, scale=float(c)))
+    def lin(o, i, c, b): call("s", [o], [i, b], lambda: g.scalar.activation(ap(o), ap(i), AF.Identity, bias=ap(b), scale=float(c)))
     def move(q, o, i, c=1.0):
         if q == "s":
             act(o, i, c)
@@ -188,6 +190,7 @@ def rank_program(g, core, T, topo):
     def trans(o, i): call("v", [o], [i], lambda: g.vector.transpose(ap(o), ap(i)))
     def col(name, j): return V(name, j, j + 1)
     def one(o, c): act(o, V("ones", 0, len(range(o[1], o[2], o[3]))), c)
+    def vec(n): return col("vecs", 16 * n + 15)
 
     roles = [rank < rank ^ s for s in STEPS]
     dma("s", ap(V("pi")), T.p[:], [V("pi")], [])
@@ -211,15 +214,12 @@ def rank_program(g, core, T, topo):
     iota(V("rows", 48, 56), [[-2, 2], [8, 4]], 2, 0)
     iota(V("rows", 82, 94), [[0, 2], [-1, 6]], 8, 0)
     iota(V("rows", 97, 111), [[0, 2], [-1, 7]], 7, 0)
-    iota(V("r16", 0, 16 * NR), [[0, NR], [1, 16]], 0, 0)
     iota(V("qk"), [[0, 8], [64, 2]], 0, 0)
-    if roles[0]:
-        iota(V("kslow"), [[0, 4], [1, 8], [0, 8]], 0, 0)
-    else:
+    if not roles[0]:
         iota(V("tfast"), [[8, 4], [0, 8], [1, 8]], 0, 0)
-    iota(V("itab"), [[0, 4], [1, 8]], 0, 0)
     iota(V("iota"), [[1, 512]], 0, 0)
     ms(V("onef"), 1.0)
+    ms(V("stg"), 0.0)
     ms(V("w"), 0.0); ms(V("b0"), 0.0); ms(V("d12"), 1.0)
     ts(V("si", 2, 3), col("si", 0), 15, A.bitwise_and)
     ts(V("si", 3, 4), col("si", 0), 7, A.bitwise_and)
@@ -244,7 +244,10 @@ def rank_program(g, core, T, topo):
     for v, a, b, s in _cover([x for r in ROWS for x in r]):
         one(V("rows", a, b, s), v)
     one(V("rows", 82, 94, 6), 4.0)
-    act(V("sel2"), I(V("s16", 16, 32), V("rep", 0, 16)), 2.0 ** -9)
+    act(V("selk"), I(V("s16", 16, 32), V("rep")))
+    act(col("pv", 7), col("pv", 8), 512.0)
+    act(col("pv", 13), col("pv", 8), -512.0)
+    act(V("sel2"), V("selk", 0, 256), 2.0 ** -9)
 
     for v in range(2):
         for e in range(2):
@@ -269,93 +272,87 @@ def rank_program(g, core, T, topo):
             one(V("d12", at, 64 * (at // 64) + 64, 16), c)
 
     def tables():
-        vec = lambda n: col("vecs", 16 * n + 15)
-        n = 16 * NR
-        ts(V("oh", 0, n), V("r16", 0, n), col("pv", 0), A.is_equal)
-        ts(V("r16", 0, n), V("r16", 0, n), 0.0, A.is_gt)
-        tt(V("oh", 0, n), V("oh", 0, n), V("rows", 0, n), A.mult)
-        ts(V("slow"), V("c2"), col("pv", 3), A.add)
-        scan(V("vecs", 0, n), V("r16", 0, n), V("oh", 0, n), A.mult, A.add)
-        ms(V("rst8"), 1.0)
+        lin(V("q32", 0, 4), V("q8", 0, 16, 4), 1.0, col("pv", 13))
+        lin(V("q32", 4, 8), V("q8", 0, 16, 4), 4.0, col("pv", 13))
         for n in range(3):
-            ts(V("il", 4 * n, 4 * n + 4), V("q8", 0, 16, 4), vec(n), A.add)
-            ts(V("kl", 4 * n, 4 * n + 4), V("q8", 0, 16, 4), vec(4 + n), A.add)
-        cp(V("il", 12, 13), vec(3))
-        ts(V("kl", 12, 13), vec(3), 1.0, A.add)
-        ms(V("rst8", 0, 256, 8), 0.0)
+            lin(S("il", 4 * n, 4 * n + 4), V("q32", 0, 4), 1.0, vec(n))
+            lin(S("kl", 4 * n, 4 * n + 4), V("q32", 0, 4), 1.0, vec(4 + n))
+        lin(S("il", 12, 13), vec(3), 1.0, col("pv", 13))
+        lin(S("slow"), V("c2"), 1.0, col("pv", 3))
+        lin(S("kl", 12, 13), S("il", 12, 13), 1.0, 1.0)
+        for k in range(2):
+            act(V("six", 256 * k, 256 * k + 256), V("ones"), 16.0)
 
     def rank_tables():
-        vec = lambda n: col("vecs", 16 * n + 15)
-        ts(col("pv", 9), col("si", 4), 32.0, A.mult)
-        ts(col("pv", 10), col("si", 3), 32.0, A.mult, 7.0, A.add)
-        ts(V("q32"), V("q8"), 4.0, A.mult)
-        ts(col("pv", 7), col("si", 2), 15.0, A.is_lt, 1024.0, A.mult)
-        ts(V("qk"), V("qk"), col("pv", 9), A.add)
-        ts(col("pv", 12), col("si", 4), 8.0, A.mult, col("pv", 10), A.add)
-        ts(V("posl"), V("q8"), col("pv", 10), A.add)
+        act(col("pv", 9), col("pv", 3), 32.0)
+        lin(col("pv", 10), col("pv", 2), 32.0, 7.0)
+        lin(col("pv", 14), col("pv", 6), 1.0, 512.0)
         for n in range(2):
-            ts(V("gl", 4 * n, 4 * n + 4), V("q32", 0, 16, 4), vec(7 + n), A.add)
-        if not all(roles):
-            ts(V("rneg8"), V("rst8"), 128.0, A.mult, -128.0, A.add)
-        ts(V("rkk"), V("qk"), vec(9), A.add)
-        ts(V("mvl"), V("c2", 0, 16, 8), col("pv", 12), A.add)
+            lin(S("gl", 4 * n, 4 * n + 4), V("q32", 4, 8), 1.0, vec(7 + n))
+        lin(V("qk"), V("qk"), 1.0, col("pv", 9))
+        lin(col("pv", 12), col("pv", 3), 8.0, col("pv", 10))
+        lin(col("pv", 15), vec(9), 1.0, col("pv", 13))
+        lin(S("posl"), V("q8"), 1.0, col("pv", 10))
         for i in range(8):
-            ts(V("rki", 2 * i, 2 * i + 2), V("qk", 0, 2), float(LOC[i]), A.add)
+            lin(S("rki", 2 * i, 2 * i + 2), V("qk", 0, 2), 1.0, float(LOC[i]))
+        lin(S("rkk"), V("qk"), 1.0, col("pv", 15))
+        lin(S("mvl"), V("c2", 0, 16, 8), 1.0, col("pv", 12))
 
-    def moved_tables():
-        ms(V("mlt", 0, 16), 0.0)
-        ts(V("mlt", 16, 32), V("s16", 0, 16), col("pv", 0), A.is_lt)
-        ms(V("erow", 0, NT), 0.0)
-        ts(V("tabd"), V("iota", 0, 32), 512.0, A.add, col("pv", 6), A.add)
+    def preparing(left, w0="w0", r0="r0"):
+        yield tt(V("dd", 0, 16), V("wd", 1, 32, 2), V("wd", 0, 32, 2), A.subtract)
+        if not left:
+            yield tt(V("nei"), I(V("wd"), V("fast")), V("tslow"), A.not_equal)
+        yield ts(V("tt"), V("dd", 0, 16), col("pv", 8), A.mult)
+        if not left:
+            yield tt(V("sig"), V("nei", 0, 256, 2), V("nei", 1, 256, 2), A.subtract)
+            yield scan(V("rsc"), V("nei"), V("ones"), A.mult, A.add)
+        yield tt(V(w0, 0, 32, 2), V("wd", 0, 32, 2), V("tt"), A.subtract)
+        if not left:
+            yield scan(V("sg2"), V("rst4"), V("sig"), A.mult, A.add)
+        yield tt(V(w0, 1, 32, 2), V("wd", 1, 32, 2), V("tt"), A.add)
+        if not left:
+            yield ts(V("r0"), V("sg2", 3, 128, 4), col("pv", 8), A.mult)
+            yield tt(V(r0), V("rsc", 7, 256, 8), V("r0"), A.subtract)
 
-    def late():
-        iota(V("idm"), [[1, 128]], 0, -1)
-        ts(V("ia"), V("hi"), 31, A.bitwise_and)
-        ts(V("ib"), V("hi"), 5, A.logical_shift_right)
-        ts(V("tabn"), V("iota", 0, 32), 16.0, A.mult, col("pv", 0), A.add)
-        ts(V("hf"), V("ia"), 16.0, A.mult)
-        ms(V("et"), 0.0)
-        tt(V("hf"), V("hf"), V("ib"), A.add)
-        for b in range(4):
-            ts(V("et", 513 * b, 512 * b + 512, 4), V("idm"), 0.0, A.is_equal, 16.0, A.mult)
-            if b == 0:
-                cp(V("hp"), V("hf"))
-        quant("e", V("et"), 0, 512)
-        act(V("hrow"), I(V("iota"), V("hp")))
-        if roles[0] and not all(roles):
-            iota(V("tslow"), [[8, 4], [1, 8], [0, 8]], 0, 0)
-            iota(V("tfast"), [[8, 4], [0, 8], [1, 8]], 0, 0)
-        if not roles[0] and any(roles):
-            iota(V("kslow"), [[0, 4], [1, 8], [0, 8]], 0, 0)
+    def state_list():
+        ts(V("h3"), V("h1"), col("base", 0), A.add, float(NT), A.is_lt)
+        yield tt(V("h4"), V("h1"), V("tabn"), A.subtract)
+        yield ts(V("h4"), V("h4"), 512.0, A.add, col("base", 0), A.add)
+        yield tt(V("h4"), V("h4"), V("h3"), A.mult)
+        yield tt(V("h4"), V("h4"), V("tabn"), A.add)
 
-    def prepare(left):
-        tt(V("dd"), V("wd", 1, 32, 2), V("wd", 0, 32, 2), A.subtract)
-        if not left:
-            tt(V("nei"), I(V("wd"), V("fast")), V("tslow"), A.not_equal)
-        ts(V("tt"), V("dd"), col("pv", 8), A.mult)
-        if not left:
-            tt(V("sig"), V("nei", 0, 256, 2), V("nei", 1, 256, 2), A.subtract)
-            scan(V("rsc"), V("nei"), V("ones"), A.mult, A.add)
-        tt(V("w0", 0, 32, 2), V("wd", 0, 32, 2), V("tt"), A.subtract)
-        if not left:
-            scan(V("sg2"), V("rst4"), V("sig"), A.mult, A.add)
-        tt(V("w0", 1, 32, 2), V("wd", 1, 32, 2), V("tt"), A.add)
-        if not left:
-            ts(V("r0"), V("sg2", 3, 128, 4), col("pv", 8), A.mult)
-            tt(V("r0"), V("rsc", 7, 256, 8), V("r0"), A.subtract)
+    def weave(*chains):
+        chains = list(chains)
+        while chains:
+            chains = [c for c in chains if next(c, 0) is None]
 
-    prepare(roles[0])
+    scan(V("vecs"), V("selk", 0, 160), V("rows"), A.add, A.max)
+    tables()
+    weave(preparing(True, w0="v0") if roles[0] else preparing(False, r0="v0"))
+    send(T.cores[rank ^ STEPS[0]], V("lv0"), V("v0"), "a9")
+    iota(V("itab"), [[0, 4], [1, 8]], 0, 0)
+    if any(roles):
+        iota(V("kslow"), [[0, 4], [1, 8], [0, 8]], 0, 0)
+    if roles[0]:
+        ts(V("dd", 16, 32), V("dd", 0, 16), -1.0, A.mult)
     for k in range(2):
         quant("x", V("x0", 1024 * k, 1024 * k + 1024), 256 * k, 256 * k + 256)
         act(V("ssb", 256 * k, 256 * k + 256), mm(k, mx("u2", 0, 128), mx("x", 256 * k, 256 * k + 256)))
     for b in range(4):
         ts(V("h0", 32 * b, 32 * b + 32), V("hi"), 4.0, A.mult, float(b), A.add)
+    ms(V("rst8"), 1.0)
+    cp(V("lists", 0, 48), V("stg", 0, 48))
+    ms(V("rst8", 0, 256, 8), 0.0)
     xcur = "x0"
     for r, step in enumerate(STEPS):
         peer = T.cores[rank ^ step]
         left = roles[r]
         last = r == len(STEPS) - 1
         snd, lnd = "snd%d" % r, V("lnd%d" % r)
+
+        def by_letter(b):
+            act(V("xl", 512 * b, 512 * b + 512), I(V(xcur), V("h1l" if r else "h0", 32 * b, 32 * b + 32)))
+
         src = "ssb"
         if r == 0:
             src = "hsc"
@@ -366,42 +363,69 @@ def rank_program(g, core, T, topo):
         for k in range(2):
             tt(V("fl", 128 * k, 128 * k + 128), I(V(src), V("al", 8 * k, 8 * k + 8)), V("bs", 128 * k, 128 * k + 128), A.is_lt)
         scan(V("fsc"), V("sel2"), V("fl"), A.add, A.max)
-        word = snd if left else "df"
-        if not left:
-            tt(V("sg1"), I(V("fsc"), V("sgl")), V("sig"), A.mult)
-        tt(V("tt"), V("fsc", 15, 256, 16), V("dd"), A.mult)
-        if not left:
-            scan(V("sg2"), V("rst4"), V("sg1"), A.mult, A.add)
-        tt(V(word, 0, 32, 2), V("w0", 0, 32, 2), V("tt"), A.add)
-        if not left:
-            tt(V(snd), V("r0"), V("sg2", 3, 128, 4), A.add)
-        tt(V(word, 1, 32, 2), V("w0", 1, 32, 2), V("tt"), A.subtract)
+        flags = V("fsc", 15, 256, 16)
+        mine = "r0" if r == 0 else snd
+        word = mine if left else "df"
+        if left and r == 0:
+            tt(V(snd, 0, 32, 2), flags, V("dd", 0, 16), A.mult)
+            tt(V(snd, 1, 32, 2), flags, V("dd", 16, 32), A.mult)
+        else:
+            if not left:
+                tt(V("sg1"), I(V("fsc"), V("sgl")), V("sig"), A.mult)
+            tt(V("tt"), flags, V("dd", 0, 16), A.mult)
+            if not left:
+                scan(V("sg2"), V("rst4"), V("sg1"), A.mult, A.add)
+            tt(V(word, 0, 32, 2), V("w0", 0, 32, 2), V("tt"), A.add)
+            if not left and r == 0:
+                cp(V(snd), V("sg2", 3, 128, 4))
+            elif not left:
+                tt(V(snd), V("r0"), V("sg2", 3, 128, 4), A.add)
+            tt(V(word, 1, 32, 2), V("w0", 1, 32, 2), V("tt"), A.subtract)
         send(peer, lnd, V(snd), "a%d" % (3 * r))
         if r == 0:
+            for b in range(4):
+                e = V("et", 512 * b, 512 * b + 512)
+                call("g", [e], [V("six")], lambda: g.affine_select(ap(e), ap(V("six")), [[-1, 512]], A.is_equal, 0.0, b, 4))
+            if roles[0] and not all(roles):
+                iota(V("tslow"), [[8, 4], [1, 8], [0, 8]], 0, 0)
+                iota(V("tfast"), [[8, 4], [0, 8], [1, 8]], 0, 0)
+            rank_tables()
             fixed()
-            tables()
-        cp(V("o1"), I(V(snd), V("il", 0, 13)))
+            tt(V(mine), V("v0"), V(snd), A.add)
+            cp(V("lists", 48, 128), V("stg", 48, 128))
+            cp(V("o1"), I(V(mine), V("il", 0, 13)))
+        else:
+            by_letter(0)
+            act(V("o1"), I(V(mine), V("il", 0, 13)))
         if left:
-            tt(V("df", 0, 31), V(snd, 0, 31), V(snd, 1, 32), A.subtract)
-        tt(V("own"), I(V(snd), V("kl", 0, 13)), V("o1"), A.is_le)
-        if left:
-            cp(V("df", 7, 32, 8), V(snd, 7, 32, 8))
+            tt(V("df", 0, 31), V(mine, 0, 31), V(mine, 1, 32), A.subtract)
+            cp(V("df", 7, 32, 8), V(mine, 7, 32, 8))
         else:
             tt(V("dtl"), I(V(word), V("slow")), V("tfast"), A.is_equal)
-        ts(V("own"), V("own"), 64.0, A.mult)
+        tt(V("own"), I(V(mine), V("kl", 0, 13)), V("o1"), A.is_le)
+        if r == 0:
+            ms(V("mlt", 0, 16), 0.0)
+        ts(V("own"), V("own"), -64.0, A.mult)
+        if r == 0:
+            ts(V("mlt", 16, 32), V("s16", 0, 16), col("pv", 0), A.is_lt)
+            tt(V("lv1"), V("lv0"), lnd, A.add)
+            lnd = V("lv1")
+            if not all(roles):
+                ts(V("rneg8"), V("rst8"), 128.0, A.mult, -128.0, A.add)
+            by_letter(0)
         if left:
-            cp(V("dtl"), I(V("df"), V("fast")))
+            act(V("dtl"), I(V("df"), V("fast")))
         else:
             for q in range(4):
-                ts(V("dtl", 64 * q, 64 * q + 64), V("dtl", 64 * q, 64 * q + 64), 64.0, A.mult, 8.0 * q - 64.0, A.add)
-        hl = "h0" if r == 0 else "h1l"
-        for b in range(4):
-            act(V("xl", 512 * b, 512 * b + 512), I(V(xcur), V(hl, 32 * b, 32 * b + 32)))
+                lin(V("dtl", 64 * q, 64 * q + 64), V("dtl", 64 * q, 64 * q + 64), 64.0, 8.0 * q - 64.0)
+        for b in range(1, 4):
+            by_letter(b)
         if r == 0:
-            rank_tables()
-            moved_tables()
-        tt(V("x1", 0, 64), I(lnd, V("il", 0, 4)), V("own", 0, 64), A.add)
-        tt(V("x1", 64, 208), I(lnd, V("il", 4, 13)), V("own", 64, 208), A.add)
+            lin(V("tabd"), V("iota", 0, 32), 1.0, col("pv", 14))
+            lin(V("tabn"), V("iota", 0, 32), 16.0, col("pv", 0))
+            act(V("erow", 0, NT), V("ones", 0, NT), 0.0)
+        tt(V("x1", 0, 64), I(lnd, V("il", 0, 4)), V("own", 0, 64), A.subtract)
+        tt(V("x1", 64, 208), I(lnd, V("il", 4, 13)), V("own", 64, 208), A.subtract)
         tt(V("b0", 0, 128, 2), I(lnd, V("kl", 0, 4)), V("x1", 0, 64), A.is_le)
         tt(V("lg", 0, 64), I(lnd, V("kl", 4, 8)), V("x1", 64, 128), A.is_le)
         scan(V("w", 128, 240), V("b0", 0, 112), V("b0", 16, 128), A.mult, A.max)
@@ -409,14 +433,15 @@ def rank_program(g, core, T, topo):
         tt(V("pp", 0, 64), I(V("w", 0, 256), V("gl", 0, 4)), V("lg", 0, 64), A.mult)
         tt(V("lg", 64, 128), I(lnd, V("kl", 8, 12)), V("x1", 128, 192), A.is_le)
         scan(V("w", 256, 384, 2), V("d12", 0, 64), V("pp", 0, 64), A.mult, A.max)
-        act(V("wi", 64, 256), I(V("w", 0, 384), V("rki", 4, 16)))
+        if r:
+            act(V("wi", 64, 256), I(V("w", 0, 384), V("rki", 4, 16)))
         tt(V("pp", 64, 128), I(V("w", 0, 384), V("gl", 4, 8)), V("lg", 64, 128), A.mult)
+        if r == 0:
+            cp(V("wi", 64, 256), I(V("w", 0, 384), V("rki", 4, 16)))
         scan(V("w", 384, 512, 2), V("d12", 64, 128), V("pp", 64, 128), A.mult, A.max)
         cp(V("wi", 0, 64), I(V("w"), V("rki", 0, 4)))
         tt(V("cmp", 64, 256), I(V("w"), V("rkk", 4, 16)), V("wi", 64, 256), A.is_gt)
         tt(V("cmp", 0, 64), I(V("w"), V("rkk", 0, 4)), V("wi", 0, 64), A.is_gt)
-        if r == 0:
-            act(V("selk"), I(V("s16", 16, 32), V("rep")))
         scan(V("pos"), V("rst8"), V("cmp"), A.mult, A.add)
         if left:
             tt(V("ne"), I(V("pos"), V("posl")), V("kslow"), A.not_equal)
@@ -430,13 +455,9 @@ def rank_program(g, core, T, topo):
         scan(V("cc"), V("onef"), V("mv"), A.mult, A.add)
         ts(V("zl"), V("nw", 7, 256, 8), col("pv", 6), A.add)
 
-        def gather_z(q, k, b):
-            move(q, V("z", 1024 * k + b, 1024 * k + 1024, 4), I(V("xl", 512 * b, 512 * b + 512), V("zl", 16 * k, 16 * k + 16)))
-
         for k in range(2):
             for b in range(4):
-                if ("g", k, b) not in LPLAN:
-                    gather_z("s", k, b)
+                act(V("z", 1024 * k + b, 1024 * k + 1024, 4), I(V("xl", 512 * b, 512 * b + 512), V("zl", 16 * k, 16 * k + 16)))
         cp(V("tot"), V("cc", 30, 32))
         ts(V("h1"), V("mv"), -2048.0, A.mult, 2047.0, A.add)
         tt(V("tr"), I(V("iota", 0, 64), V("tot")), V("mlt"), A.mult)
@@ -449,9 +470,7 @@ def rank_program(g, core, T, topo):
         outs = {}
         for what, k, b in LPLAN:
             piece = V("z32", 512 * b + 256 * k, 512 * b + 256 * k + 256)
-            if what == "g":
-                gather_z("v", k, b)
-            elif what == "q":
+            if what == "q":
                 quant("z", V("z", 1024 * k, 1024 * k + 1024), 256 * k, 256 * k + 256)
                 outs[k] = [mm(4 * k + n, mx("w", 128 * n, 128 * n + 128), mx("z", 256 * k, 256 * k + 256)) for n in range(4)]
             elif what in "zs":
@@ -464,41 +483,47 @@ def rank_program(g, core, T, topo):
                 ts(V("el"), V("esc", 15, NT, 16), col("pv", 7), A.subtract)
         for q, b, c0, c1 in FPLAN:
             move(q, V("ft", 64 * c0 + b, 64 * c1, 4), I(V("yg", YW * b, YW * b + C), V("el", c0, c1)), 2.0 ** -5)
+        if r == 0:
+            ts(V("ia"), V("hi"), 31, A.bitwise_and)
+            ts(V("ib"), V("hi"), 5, A.logical_shift_right)
         quant("f%d" % r, V("ft"), 0, NT)
         send(peer, V("lq%d" % r), V("qf%d" % r), "a%d" % (3 * r + 1), dt.uint8)
         send(peer, V("ls%d" % r), V("sf%d" % r), "a%d" % (3 * r + 2))
         if r == 0:
-            late()
-        ts(V("h3"), V("h1"), col("base", 0), A.add, float(NT), A.is_lt)
-        tt(V("h4"), V("h1"), V("tabn"), A.subtract)
-        ts(V("f16"), V("ft"), 16.0, A.mult)
-        ts(V("h4"), V("h4"), 512.0, A.add, col("base", 0), A.add)
-        tt(V("h4"), V("h4"), V("h3"), A.mult)
-        tt(V("h4"), V("h4"), V("tabn"), A.add)
+            ts(V("hf"), V("ia"), 16.0, A.mult)
+            act(V("f16"), V("ft"), 16.0)
+            tt(V("hf"), V("hf"), V("ib"), A.add)
+            cp(V("hp"), V("hf"))
+            act(V("hrow"), I(V("iota"), V("hp")))
+            quant("e", V("et"), 0, 512)
         if not last:
-            cp(V("xll"), V("h4"))
             act(V("hw"), I(V("hrow"), V("zl")))
-            prepare(roles[r + 1])
-            scan(V("hsc"), V("selk"), V("hw"), A.add, A.max)
+        if r:
+            act(V("f16"), V("ft"), 16.0)
+        if not last:
+            weave(state_list(), preparing(roles[r + 1]))
+            cp(V("xll"), V("h4"))
             if r == 0:
                 for b in range(4):
                     ts(V("h1l", 32 * b, 32 * b + 32), V("hf"), 4.0, A.mult, float(b), A.add)
-            else:
-                quant("v", V("vt"), 0, 128)
-            ts(V("al"), V("hsc", 15, 512, 32), col("pv", 7), A.subtract)
-            ts(V("bl"), V("hsc", 31, 512, 32), col("pv", 7), A.subtract)
+            scan(V("hsc"), V("selk"), V("hw"), A.add, A.max)
         else:
+            weave(state_list())
             for v in range(2):
                 for e in range(2):
                     ts(V("t64", 32 * v + 16 * e, 32 * v + 16 * e + 16), V("h4", 16 * v, 16 * v + 16), col("pv", 4 + e), A.mult)
+            ts(V("opf"), V("wd"), col("pv", 6), A.add)
             trans(V("u64"), V("t64"))
+            quant("v", V("vt"), 0, 128)
             for v in range(2):
                 tt(V("h3", v, 32, 2), V("u64", 32 * v, 32 * v + 16), V("u64", 32 * v + 16, 32 * v + 32), A.add)
             cp(V("xll"), V("h3"))
-            ts(V("opf"), V("wd"), col("pv", 6), A.add)
             dma("y", T.op[:], ap(V("opf")), [], [V("opf")])
         for b in range(4):
             o = mm(4 + b, mx("e", 128 * b, 128 * b + 128), (V("lq%d" % r), V("ls%d" % r)))
+            if b == 0 and not last:
+                ts(V("al"), V("hsc", 15, 512, 32), col("pv", 7), A.subtract)
+                ts(V("bl"), V("hsc", 31, 512, 32), col("pv", 7), A.subtract)
             tt(V("yg", YW * b + C, YW * b + YW), o, V("f16", b, 4 * NT, 4), A.add)
         xcur = "xa"
         bank, after = 0, []

@@ -12,64 +12,52 @@ def _buf(name, n, dtype, where="sbuf"):
 
 
 for _n, _w in [("x0", 2048), ("xa", 2048), ("xl", 2048), ("z", 2048), ("z32", 2048), ("yg", 4 * YW), ("ft", 4 * NT), ("f16", 4 * NT), ("ut", 512), ("vt", 512),
-               ("et", 2048), ("six", 512), ("fl", 256), ("fsc", 256), ("sel2", 256), ("w", 512), ("b0", 128), ("lg", 128), ("d12", 256), ("pp", 128), ("x1", 208),
-               ("o1", 208), ("own", 208), ("wi", 256), ("cmp", 256), ("pos", 256), ("ne", 256), ("nw", 256), ("dtl", 256), ("kslow", 256), ("tfast", 256),
-               ("tslow", 256), ("rst8", 256), ("rneg8", 256), ("rst4", 128), ("ones", 256), ("sig", 128), ("sg1", 128), ("sg2", 128), ("nei", 256), ("rsc", 256),
-               ("wd", 32), ("w0", 32), ("r0", 32), ("df", 32), ("dd", 32), ("v0", 32), ("lv0", 32), ("lv1", 32), ("tt", 16), ("itab", 32)]:
+               ("et", 528), ("fl", 256), ("fsc", 256), ("sel2", 256), ("w", 640), ("b0", 144), ("lg", 128), ("d12", 256), ("pp", 128), ("x1", 208),
+               ("o1", 208), ("own", 208), ("ob", 208), ("gap", 256), ("turn", 256), ("far", 256), ("wi", 256), ("cmp", 256), ("pos", 256), ("ne", 256), ("nw", 256),
+               ("dtl", 256), ("kslow", 256), ("kback", 256), ("tslow", 256), ("rst8", 256), ("rst4", 128), ("ones", 256), ("sig", 128), ("sg1", 128), ("sg2", 128),
+               ("nei", 256), ("rsc", 256), ("wd", 32), ("w0", 32), ("r0", 32), ("df", 32), ("dd", 32), ("m64", 32), ("lv1", 32), ("tt", 16), ("itab", 32)]:
     _buf(_n, _w, "bfloat16")
 for _r in range(3):
-    _buf("snd%d" % _r, 32, "bfloat16"); _buf("lnd%d" % _r, 32, "bfloat16")
+    _buf("snd%d" % _r, 64, "bfloat16"); _buf("lnd%d" % _r, 64, "bfloat16")
     _buf("qf%d" % _r, NT, CODE); _buf("sf%d" % _r, NT, "uint8"); _buf("lq%d" % _r, NT, CODE); _buf("ls%d" % _r, NT, "uint8")
 for _n, _w in [("qx", 512), ("qz", 512), ("qw", 512), ("qe", 512), ("qu", 128), ("qu2", 128), ("qv", 128)]:
     _buf(_n, _w, CODE); _buf("s" + _n[1:], _w, "uint8")
-for _n, _w in [("ssb", 512), ("bs", 256), ("iota", 512), ("selk", 512), ("erow", 1536), ("esc", NT), ("hrow", 512), ("hw", 512), ("hsc", 512), ("yo", 512),
-               ("pv", 16), ("s16", 48), ("rows", 160), ("stg", 128), ("vecs", 160), ("q8", 16), ("q32", 16), ("c2", 16),
-               ("t64", 64), ("u64", 64), ("mv", 32), ("cc", 32), ("h1", 32), ("h3", 32), ("h4", 32), ("tabn", 32), ("tabd", 32), ("mlt", 32), ("tr", 32),
-               ("base", 2), ("opf", 32), ("onef", 32), ("hf", 32), ("qk", 16)]:
+for _n, _w in [("ssb", 512), ("bs", 256), ("iota", 512), ("place", 512), ("selk", 512), ("erow", 2048), ("esc", NT), ("hrow", 512), ("hw", 512), ("hsc", 512), ("yo", 512),
+               ("pv", 16), ("s16", 48), ("rows", 192), ("stg", 128), ("vecs", 192), ("h4b", 128), ("q8", 16), ("c2", 16), ("i64", 64),
+               ("t64", 64), ("u64", 64), ("mv", 32), ("cc", 32), ("h1", 32), ("h3", 32), ("h4", 32), ("tabn", 32), ("tabd", 34), ("vc", 12), ("mlt", 32), ("tr", 32),
+               ("base", 4), ("opf", 32), ("hf", 32), ("qk", 16)]:
     _buf(_n, _w, "float32")
 for _n, _w in [("pi", 32), ("hi", 32), ("ia", 32), ("ib", 32), ("si", 8)]:
     _buf(_n, _w, "int32")
-for _n, _w in [("il", 14), ("kl", 14), ("slow", 16), ("gl", 8), ("rkk", 16), ("rki", 16), ("posl", 16), ("mvl", 2), ("fast", 16), ("sgl", 8), ("rep", 32),
-               ("h0", 128), ("h1l", 128), ("hn", 32), ("hp", 32), ("zl", 32), ("al", 16), ("bl", 16), ("tot", 2), ("dst", 32), ("el", 14), ("xll", 32)]:
+for _n, _w in [("il", 14), ("kl", 14), ("gl", 8), ("late", 16), ("soon", 16), ("posl", 16), ("mvl", 2), ("pad", 16), ("fast", 16), ("sgl", 8), ("rep", 32),
+               ("h0", 128), ("h1l", 128), ("hn", 32), ("zl", 32), ("al", 16), ("bl", 16), ("tot", 2), ("dst", 32), ("el", 14), ("xll", 32)]:
     POOL[_n] = ("lists", _at[0], _w)
     _at[0] += -(-_w // 16) * 16
 _buf("lists", _at[0], "uint16")
 _buf("ul", 8, "uint16")
 _buf("ps", 4096, "float32", "psum")
-SEMAPHORES = ["qv", "qs", "qt", "qg", "sent"] + ["d%d" % i for i in range(24)] + ["a%d" % i for i in range(10)]
+SEMAPHORES = ["qv", "qs", "qt", "qg", "sent"] + ["d%d" % i for i in range(24)] + ["a%d" % i for i in range(12)]
 
 F = [1.25, 1.5, 2.0, 4.0, 16.0, 256.0, 2.0 ** 16, 2.0 ** 32]
-GI = [[0, 5, 4, 0, 0, 4, 0, 0, 6, 5, 4, 0, 6, 4, 0, 0], [0, 0, 3, 3, 3, 3, 3, 3, 2, 2, 2, 2, 2, 3, 0, 0], [1, 1, 1, 1, 1, 1, 1, 1, 0, 0, 0, 0, 0, 0, 1, 0]]
-GK0 = [0, 6, 5, 0, 0, 6, 0, 0, 7, 7, 7, 7, 7, 7, 0, 0]
-W7, B3, B2, B1, B0 = 0, 1, 2, 3, 4
-W6, W5, W4A, W4B = 129, 131, 133, 139
-W4, W3, W2, W1, W0 = 258, 270, 282, 398, 412
-LOC = [W0, W1, W2, W3, W4, W5, W6, W7]
-P1 = [W4A, W4B, W4B, W7, W6, W5, W4A, B3, W4B, W7, W6, W5, W4A, B2, W7, W7]
-P2 = [W7, W7, W6, W5, W4, W3, W2, B1, W7, W6, W5, W4, W3, W2, B0, W7]
-NONE = [0] * 16
-ROWS = GI + [NONE, GK0, NONE, NONE, P1, P2, LOC + LOC]
-LPLAN = [(w[0], int(w[1]), int(w[2])) for w in "q00 z00 z01 z02 s10 s11 s12 s03 s13 e00 a00 q10 l00 a01 a10 a11 a02 a12 a03 a13".split()]
-FPLAN = [("s", 0, 0, 14), ("s", 1, 0, 14), ("s", 2, 0, 14), ("v", 3, 0, 8), ("s", 3, 8, 14)]
-XPLAN = [("s", 0, 288, 0), ("s", 0, 288, 1), ("s", 0, 288, 2), ("v", 0, 288, 3), ("s", 288, 512, 0), ("s", 288, 512, 1), ("v", 288, 512, 3), ("q", 0, 288, "s"),
-         ("v", 288, 512, 2), ("q", 288, 512, "v")]
+B3, B2, B1, B0 = 1, 2, 3, 4
+W7, W6, W5, W4A, NIL, W4B = 127, 129, 131, 133, 135, 139
+W4, W3, W2, YES, NO, W1, W0, HUGE = 258, 272, 286, 385, 386, 526, 542, 2.0 ** 40
+PAIRS = [(34, 42, 1, 3, 0), (42, 48, 1, 2, 0), (50, 53, 1, 7, -1), (58, 62, 1, 7, -1), (62, 63, 1, 4, 0), (56, 64, 7, 3, -1),
+         (64, 72, 1, 1, 0), (81, 88, 1, 7, -1), (89, 95, 1, 7, -1), (5, 16, 8, 4, 0), (24, 32, 1, 7, 0)]
+PLACES = [(129, 132, 1, W7, 2), (132, 135, 1, W4, 14), (122, 126, 1, W7, 2), (114, 117, 1, W7, 2), (136, 144), (112, 128, 14, W4B, 0), (113, 114, 1, W4A, 0), (144, 160),
+          (120, 128, 7, B3, 1), (160, 192), (135, 144, 8, B1, 1), (144, 160, 8, W1, 0), (151, 160, 8, W0, 0), (167, 176, 8, YES, 0), (176, 192, 8, NO, 0)]
+X0 = [(0, 384), (384, 512)]
+ROWS_EARLY, FIXED_EARLY, LISTS_EARLY, LISTS_NEXT = 20, 17, 4, 22
+LPLAN = ("ne0 mv nw0 cc zl0 gs00 gs01 gs02 gs03 ha tot ne1 tr hb nw1 base zl1 gs10 gs11 gs12 gs13 dst zv00 sc q0 esc zv03 zv02 el q1 "
+         "zs01 zs10 zs11 zs12 zs13 a00 a01 a10 a11 a02 a12 a03 a13 fs00e fs10e fs20e fv308 fs38e").split()
 
 
-def _cover(vals):
-    out = []
-    for v in sorted(set(vals) - {0}):
-        left = [i for i, x in enumerate(vals) if x == v]
-        while left:
-            best = [left[0]]
-            for s in range(1, len(vals)):
-                run = [left[0]]
-                while run[-1] + s in left:
-                    run.append(run[-1] + s)
-                if len(run) > len(best):
-                    best = run
-            out.append((v, best[0], best[-1] + 1, best[1] - best[0] if len(best) > 1 else 1))
-            left = [i for i in left if i not in best]
-    return out
+def _pieces(cuts, plan):
+    return [(w[0], cuts[int(w[1])], cuts[int(w[1]) + 1], w[2] if w[0] == "q" else int(w[2])) for w in plan.split()]
+
+
+XPLAN = _pieces((0, 192, 384, 512), "s00 s01 s02 v12 v03 s10 s11 v13 q0s s21 s20 v23 v22 q1s q2v")
+XLAST = _pieces((0, 288, 512), "s00 s01 s02 v03 s10 s11 v13 q0s v12 q1v")
 
 
 def rank_program(g, core, T, topo):
@@ -152,13 +140,15 @@ def rank_program(g, core, T, topo):
         Q[q].dma_start(out, in_).then_inc(T.sem[tok[0]], 16)
         total[tok[0]] = 16
 
-    def send(peer, dst, src, sem, cast=None):
-        rid, pid, _e = topo.addr(peer)
-        total["sent"] = total.get("sent", 0) + len(topo.engines(core, peer))
-        order("g", [], [src], ("sent", 0))
-        g.remote_dma(ap(dst, cast), ap(src, cast), T.sem[sem], T.sem.sent, pid, rid, topo.mask(core, peer))
-        total[sem] = len(topo.engines(peer, core))
-        log[dst[0]] = [(cols(dst), True, (sem, total[sem]))]
+    def send(peer, dst, src, sem, cast=None, writes=True, gets=True):
+        if writes:
+            rid, pid, _e = topo.addr(peer)
+            total["sent"] = total.get("sent", 0) + len(topo.engines(core, peer))
+            order("g", [], [src], ("sent", 0))
+            g.remote_dma(ap(dst, cast), ap(src, cast), T.sem[sem], T.sem.sent, pid, rid, topo.mask(core, peer))
+        if gets:
+            total[sem] = len(topo.engines(peer, core))
+            log.setdefault(dst[0], []).append((cols(dst), True, (sem, total[sem])))
 
     def cp(o, i): call("v", [o], [i], lambda: g.vector.tensor_copy(ap(o), ap(i)))
     def tt(o, a, b, op): call("v", [o], [a, b], lambda: g.vector.tensor_tensor(ap(o), ap(a), ap(b), op))
@@ -167,7 +157,7 @@ def rank_program(g, core, T, topo):
             call("v", [o], [a, s1], lambda: g.vector.tensor_scalar(ap(o), ap(a), ap(s1), None, op))
         else:
             call("v", [o], [a, s1, s2], lambda: g.vector.tensor_scalar(ap(o), ap(a), ap(s1), ap(s2), op, op1))
-    def scan(o, a, b, op0, op1): call("v", [o], [a, b], lambda: g.vector.tensor_tensor_scan(ap(o), ap(a), ap(b), 0.0, op0, op1))
+    def scan(o, a, b, op0, op1, first=0.0): call("v", [o], [a, b, first], lambda: g.vector.tensor_tensor_scan(ap(o), ap(a), ap(b), ap(first), op0, op1))
     def ms(o, c): call("v", [o], [], lambda: g.vector.memset(ap(o), c))
     def act(o, i, c=1.0): call("s", [o], [i], lambda: g.scalar.activation(ap(o), ap(i), AF.Copy, scale=float(c)))
     def lin(o, i, c, b): call("s", [o], [i, b], lambda: g.scalar.activation(ap(o), ap(i), AF.Identity, bias=ap(b), scale=float(c)))
@@ -187,168 +177,194 @@ def rank_program(g, core, T, topo):
     def iota(o, pat, base, cm):
         small = SCRATCH[o[0]][2] != "int32"
         call("g", [o], [], lambda: g.iota(ap(o), pat, base, cm, allow_small_or_imprecise_dtypes=True) if small else g.iota(ap(o), pat, base, cm))
+    def select(o, i, pat, op, other, base, cm): call("g", [o], [i], lambda: g.affine_select(ap(o), ap(i), pat, op, float(other), base, cm))
     def trans(o, i): call("v", [o], [i], lambda: g.vector.transpose(ap(o), ap(i)))
     def col(name, j): return V(name, j, j + 1)
-    def one(o, c): act(o, V("ones", 0, len(range(o[1], o[2], o[3]))), c)
-    def vec(n): return col("vecs", 16 * n + 15)
-
-    roles = [rank < rank ^ s for s in STEPS]
-    dma("s", ap(V("pi")), T.p[:], [V("pi")], [])
-    dma("y", ap(V("ut")), T.u[:], [V("ut")], [])
-    dma("s", ap(V("hi")), T.h[:], [V("hi")], [])
-    for k in range(2):
-        dma("y", ap(V("x0", 1024 * k, 1024 * k + 1024)), T.x[:, 1024 * k:1024 * k + 1024], [V("x0", 1024 * k, 1024 * k + 1024)], [])
-    dma("y", ap(V("qw"), dt.uint8), T.wc[:], [V("qw")], [V("x0")])
-    dma("y", ap(V("sw")), T.ws[:], [V("sw")], [])
-    dma("y", ap(V("vt")), T.v[:], [V("vt")], [])
-
-    ms(V("ones"), 1.0)
-    ms(V("rows"), 0.0)
-    iota(V("si", 0, 2), [[0, 2]], 0, 1)
-    iota(V("s16", 0, 16), [[1, 16]], 0, 0)
-    iota(V("ia", 0, 8), [[16, 8]], 0, 0)
-    iota(V("q8"), [[8, 4], [0, 4]], 0, 0)
-    if not roles[0]:
-        iota(V("tslow"), [[8, 4], [1, 8], [0, 8]], 0, 0)
-    iota(V("c2"), [[2, 16]], 0, 0)
-    iota(V("rows", 48, 56), [[-2, 2], [8, 4]], 2, 0)
-    iota(V("rows", 82, 94), [[0, 2], [-1, 6]], 8, 0)
-    iota(V("rows", 97, 111), [[0, 2], [-1, 7]], 7, 0)
-    iota(V("qk"), [[0, 8], [64, 2]], 0, 0)
-    if not roles[0]:
-        iota(V("tfast"), [[8, 4], [0, 8], [1, 8]], 0, 0)
-    iota(V("iota"), [[1, 512]], 0, 0)
-    ms(V("onef"), 1.0)
-    ms(V("stg"), 0.0)
-    ms(V("w"), 0.0); ms(V("b0"), 0.0); ms(V("d12"), 1.0)
-    ts(V("si", 2, 3), col("si", 0), 15, A.bitwise_and)
-    ts(V("si", 3, 4), col("si", 0), 7, A.bitwise_and)
-    ts(V("si", 4, 5), col("si", 0), 3, A.logical_shift_right, 1, A.bitwise_and)
-    ts(V("si", 5, 6), col("si", 0), 4, A.logical_shift_right, 1, A.bitwise_and)
-    ts(V("si", 6, 7), col("si", 0), 3, A.bitwise_and)
-    cp(V("ul"), V("ia", 0, 8))
-    cp(col("pv", 0), col("si", 2)); cp(V("pv", 2, 4), V("si", 3, 5)); cp(col("pv", 5), col("si", 5))
-    ts(col("pv", 1), col("si", 2), 1.0, A.add)
-    ts(col("pv", 4), col("si", 5), -1.0, A.mult, 1.0, A.add)
-    ts(col("pv", 6), col("si", 2), 32.0, A.mult)
-    ts(col("pv", 8), col("si", 2), 15.0, A.is_lt, 2.0, A.mult)
-    ts(col("pv", 11), col("si", 6), 16.0, A.mult, 15.0, A.add)
-    ts(V("s16", 16, 32), V("s16", 0, 16), col("pv", 0), A.is_equal, -4096.0, A.mult)
-    ts(V("s16", 32, 48), V("s16", 0, 16), col("pv", 1), A.is_equal, 1024.0, A.mult)
-    ts(V("rep"), V("onef"), col("pv", 0), A.mult)
-    tt(V("s16", 16, 32), V("s16", 16, 32), V("s16", 32, 48), A.add)
-    ts(V("fast"), V("q8"), col("pv", 2), A.add)
-    ms(V("rst4"), 1.0)
-    ts(V("sgl"), V("q8", 0, 16, 2), 8.0, A.mult, col("pv", 11), A.add)
-    ms(V("rst4", 0, 128, 4), 0.0)
-    for v, a, b, s in _cover([x for r in ROWS for x in r]):
-        one(V("rows", a, b, s), v)
-    one(V("rows", 82, 94, 6), 4.0)
-    act(V("selk"), I(V("s16", 16, 32), V("rep")))
-    act(col("pv", 7), col("pv", 8), 512.0)
-    act(col("pv", 13), col("pv", 8), -512.0)
-    act(V("sel2"), V("selk", 0, 256), 2.0 ** -9)
-
-    for v in range(2):
-        for e in range(2):
-            ts(V("t64", 32 * v + 16 * e, 32 * v + 16 * e + 16), V("pi", v, 32, 2), col("pv", 4 + e), A.mult)
-    trans(V("u64"), V("t64"))
-    for v in range(2):
-        tt(V("opf", 16 * v, 16 * v + 16), V("u64", 32 * v, 32 * v + 16), V("u64", 32 * v + 16, 32 * v + 32), A.add)
-    quant("u", V("ut"), 0, 128)
-    ts(V("wd"), V("opf"), col("pv", 6), A.subtract)
-    cp(V("al"), V("opf", 0, 32, 2)); cp(V("bl"), V("opf", 1, 32, 2))
-    call("v", [V("qu2")], [I(V("qu"), V("ul"))], lambda: g.vector.tensor_copy(ap(V("qu2"), dt.uint32), ap(I(V("qu"), V("ul")), dt.uint32)))
-    call("s", [V("su2")], [I(V("su"), V("ul"))], lambda: g.scalar.activation(ap(V("su2")), ap(I(V("su"), V("ul"))), AF.Copy))
-    cp(V("hn"), V("hi"))
+    def ones(o): return V("ones", 0, len(range(o[1], o[2], o[3])))
+    def one(o, c): act(o, ones(o), c)
+    def fill(o, c): select(o, ones(o), [[0, ones(o)[2]]], A.is_equal, c, 1, 0)
+    def resets(o, n): select(o, ones(o), [[0, o[2] // n], [1, n]], A.not_equal, 0.0, 0, 0)
+    def vec(n): return col("vc", n)
 
     def fixed():
-        one(V("w", W7, 128, 32), 1.0)
-        for at, i in ((B3, 3), (B2, 2), (B1, 1), (B0, 0)):
-            one(V("w", at, 128, 32), F[i] / F[7])
         for at, i in ((1, 6), (3, 5), (5, 4), (9, 6), (11, 4)):
-            one(V("b0", at, 128, 32), F[i]); one(V("b0", 16 + at, 128, 32), F[i] / F[7])
-        for at, c in ((0, 0.0), (2, 0.0), (7, F[3]), (13, F[2]), (14, 0.0), (64, 0.0), (65, 0.0), (71, F[1]), (78, F[0]), (79, 0.0)):
-            one(V("d12", at, 64 * (at // 64) + 64, 16), c)
+            yield fill(V("b0", 16 + at, 144, 32), F[i])
+            yield fill(V("b0", 32 + at, 144, 32), F[i] / F[7])
+        yield fill(V("b0", 31, 144, 32), 1.0)
+        for at, i in ((B3, 3), (B2, 2), (B1, 1), (B0, 0)):
+            yield fill(V("w", at, 128, 32), F[i] / F[7])
+        for at, c in ((0, 0.0), (8, F[3]), (15, F[2]), (65, 0.0), (72, F[1]), (80, F[0])):
+            yield fill(V("d12", at, 64 if at < 64 else 129, 16), c)
+
+    def paint(runs):
+        for run in runs:
+            if len(run) == 2:
+                yield act(V("rows", *run), V("rows", 128, 128 + run[1] - run[0]))
+            else:
+                o = V("rows", *run[:3])
+                yield lin(o, V("s16", 0, ones(o)[2]), run[4], float(run[3]))
 
     def tables():
-        lin(V("q32", 0, 4), V("q8", 0, 16, 4), 1.0, col("pv", 13))
-        lin(V("q32", 4, 8), V("q8", 0, 16, 4), 4.0, col("pv", 13))
+        yield act(col("pv", 13), col("pv", 8), -512.0)
+        yield act(col("pv", 9), col("pv", 2), 32.0)
+        yield lin(V("vc"), V("vecs", 15, 192, 16), 1.0, col("pv", 13))
+        yield lin(V("qk"), V("qk"), 1.0, col("pv", 9))
         for n in range(3):
-            lin(S("il", 4 * n, 4 * n + 4), V("q32", 0, 4), 1.0, vec(n))
-            lin(S("kl", 4 * n, 4 * n + 4), V("q32", 0, 4), 1.0, vec(4 + n))
-        lin(S("il", 12, 13), vec(3), 1.0, col("pv", 13))
-        lin(S("slow"), V("c2"), 1.0, col("pv", 3))
-        lin(S("kl", 12, 13), S("il", 12, 13), 1.0, 1.0)
-        for k in range(2):
-            act(V("six", 256 * k, 256 * k + 256), V("ones"), 16.0)
-
-    def rank_tables():
-        act(col("pv", 9), col("pv", 3), 32.0)
-        lin(col("pv", 10), col("pv", 2), 32.0, 7.0)
-        lin(col("pv", 14), col("pv", 6), 1.0, 512.0)
+            yield lin(S("il", 4 * n, 4 * n + 4), V("q8", 0, 16, 4), 1.0, vec(2 * n))
+            yield lin(S("kl", 4 * n, 4 * n + 4), V("q8", 0, 16, 4), 1.0, vec(2 * n + 1))
+        yield act(S("il", 12, 13), vec(6))
+        yield lin(S("kl", 12, 13), vec(6), 1.0, 1.0)
         for n in range(2):
-            lin(S("gl", 4 * n, 4 * n + 4), V("q32", 4, 8), 1.0, vec(7 + n))
-        lin(V("qk"), V("qk"), 1.0, col("pv", 9))
-        lin(col("pv", 12), col("pv", 3), 8.0, col("pv", 10))
-        lin(col("pv", 15), vec(9), 1.0, col("pv", 13))
-        lin(S("posl"), V("q8"), 1.0, col("pv", 10))
-        for i in range(8):
-            lin(S("rki", 2 * i, 2 * i + 2), V("qk", 0, 2), 1.0, float(LOC[i]))
-        lin(S("rkk"), V("qk"), 1.0, col("pv", 15))
-        lin(S("mvl"), V("c2", 0, 16, 8), 1.0, col("pv", 12))
+            yield lin(S("gl", 4 * n, 4 * n + 4), V("q8", 0, 16, 4), 4.0, vec(7 + n))
+        for j in range(2):
+            yield lin(S("soon", j, 12, 2), V("rows", 129, 135), 1.0, col("qk", j))
+            yield lin(S("soon", 12 + 2 * j, 14 + 2 * j), V("qk", 0, 2), 1.0, vec(10 + j))
+            yield lin(S("late", 12 + 2 * j, 14 + 2 * j), V("qk", 0, 2), 1.0, float((W1, W0)[j]))
+        yield lin(col("pv", 10), col("pv", 1), -32.0, 231.0)
+        yield lin(S("late", 0, 12), V("qk", 0, 12), 1.0, vec(9))
+        yield lin(col("pv", 12), col("pv", 2), 8.0, col("pv", 10))
+        yield lin(S("posl"), V("q8"), 1.0, col("pv", 10))
+        yield lin(S("mvl"), V("c2", 0, 16, 8), 1.0, col("pv", 12))
 
-    def preparing(left, w0="w0", r0="r0"):
-        yield tt(V("dd", 0, 16), V("wd", 1, 32, 2), V("wd", 0, 32, 2), A.subtract)
-        if not left:
-            yield tt(V("nei"), I(V("wd"), V("fast")), V("tslow"), A.not_equal)
-        yield ts(V("tt"), V("dd", 0, 16), col("pv", 8), A.mult)
-        if not left:
-            yield tt(V("sig"), V("nei", 0, 256, 2), V("nei", 1, 256, 2), A.subtract)
-            yield scan(V("rsc"), V("nei"), V("ones"), A.mult, A.add)
-        yield tt(V(w0, 0, 32, 2), V("wd", 0, 32, 2), V("tt"), A.subtract)
-        if not left:
-            yield scan(V("sg2"), V("rst4"), V("sig"), A.mult, A.add)
-        yield tt(V(w0, 1, 32, 2), V("wd", 1, 32, 2), V("tt"), A.add)
-        if not left:
-            yield ts(V("r0"), V("sg2", 3, 128, 4), col("pv", 8), A.mult)
-            yield tt(V(r0), V("rsc", 7, 256, 8), V("r0"), A.subtract)
+    def gaps():
+        lin(col("pv", 14), col("pv", 8), 1.0, 0.5)
+        one(V("gap", 1, 256, 2), 4.0)
+        lin(col("pv", 15), col("pv", 8), 2.0, 1.0)
+        lin(col("base", 2), col("pv", 8), -2.0, 1.0)
+        act(col("base", 3), col("pv", 8), -1.0)
+        for o, c in ((V("gap", 0, 256, 2), col("pv", 14)), (V("turn", 0, 256, 2), col("pv", 15)), (V("turn", 1, 256, 2), col("base", 2))):
+            lin(o, ones(o), 0.0, c)
+
+    def preparing(r):
+        if roles[r]:
+            w0, at = ("w0", 0) if r else ("snd0", 32)
+            yield tt(V("dd", 0, 16), V("wd", 1, 32, 2), V("wd", 0, 32, 2), A.subtract)
+            yield ts(V("tt"), V("dd", 0, 16), col("pv", 8), A.mult)
+            yield tt(V(w0, at, at + 32, 2), V("wd", 0, 32, 2), V("tt"), A.subtract)
+            yield tt(V(w0, at + 1, at + 32, 2), V("wd", 1, 32, 2), V("tt"), A.add)
+            return
+        yield tt(V("nei"), I(V("wd"), V("fast")), V("tslow"), A.not_equal)
+        yield None
+        yield scan(V("far"), V("nei"), V("gap"), A.mult, A.add)
+        yield tt(V("sig"), V("nei", 0, 256, 2), V("nei", 1, 256, 2), A.subtract)
+        yield cp(V("snd%d" % r, 32, 64), V("far", 7, 256, 8))
+        yield scan(V("rsc"), V("nei"), V("turn"), A.mult, A.add)
+
+    def early(r):
+        send(T.cores[rank ^ STEPS[r]], V("lnd%d" % r, 32, 64), V("snd%d" % r, 32, 64), "a%d" % (9 + r), writes=r == 0 or not roles[r], gets=r == 0 or roles[r])
 
     def state_list():
-        ts(V("h3"), V("h1"), col("base", 0), A.add, float(NT), A.is_lt)
-        yield tt(V("h4"), V("h1"), V("tabn"), A.subtract)
-        yield ts(V("h4"), V("h4"), 512.0, A.add, col("base", 0), A.add)
-        yield tt(V("h4"), V("h4"), V("h3"), A.mult)
-        yield tt(V("h4"), V("h4"), V("tabn"), A.add)
+        act(V("wd"), V("nw", 7, 256, 8))
+        lin(col("base", 1), col("base", 0), 1.0, float(C))
+        lin(col("base", 2), col("base", 0), -4096.0, 4096.0 * (NT - 0.5))
+        lin(V("h3"), V("h1"), 1.0, col("base", 1))
+        lin(V("h4"), V("h1"), -4096.0, col("base", 2))
+        yield None
+        yield tt(V("h4"), V("h4"), V("h3"), A.min)
+        yield tt(V("h4"), V("h4"), V("tabn"), A.max)
 
     def weave(*chains):
         chains = list(chains)
         while chains:
             chains = [c for c in chains if next(c, 0) is None]
 
-    scan(V("vecs"), V("selk", 0, 160), V("rows"), A.add, A.max)
-    tables()
-    weave(preparing(True, w0="v0") if roles[0] else preparing(False, r0="v0"))
-    send(T.cores[rank ^ STEPS[0]], V("lv0"), V("v0"), "a9")
-    iota(V("itab"), [[0, 4], [1, 8]], 0, 0)
-    if any(roles):
-        iota(V("kslow"), [[0, 4], [1, 8], [0, 8]], 0, 0)
+    def some(chain, n):
+        for _ in range(n):
+            next(chain, 0)
+
+    roles = [rank < rank ^ s for s in STEPS]
+    dma("s", ap(V("pi")), T.p[:], [V("pi")], [])
+    dma("y", ap(V("ut")), T.u[:], [V("ut")], [])
+    for a, e in X0:
+        dma("y", ap(V("x0", 4 * a, 4 * e)), T.x[:, 4 * a:4 * e], [V("x0", 4 * a, 4 * e)], [])
+    dma("y", ap(V("hi")), T.h[:], [V("hi")], [])
+
+    iota(V("si", 0, 2), [[0, 2]], 0, 1)
+    iota(V("s16", 0, 32), [[-1, 2], [1, 16]], 0, 0)
+    iota(V("q8"), [[8, 4], [0, 4]], 0, 0)
+    iota(V("ia", 0, 8), [[16, 8]], 0, 0)
+    if not roles[0]:
+        iota(V("tslow"), [[8, 4], [1, 8], [0, 8]], 0, 0)
+    ms(V("ones"), 1.0)
+    one(V("rows", 32, 96), 0.0)
+    one(V("rows", 112, 136), NIL)
+    one(V("stg"), 0.0)
+    iota(V("rows", 0, 32), [[1, 2], [0, 4], [-1, 4]], 6, 0)
+    iota(V("rows", 96, 112), [[-2, 2], [8, 4], [-1, 2]], 3, 0)
+    iota(V("c2"), [[2, 16]], 0, 0)
+    iota(V("qk"), [[0, 8], [64, 2]], 0, 0)
+    iota(V("i64"), [[1, 64]], 0, 0)
+    resets(V("rst4"), 4)
+    if not all(roles):
+        iota(V("kback"), [[0, 4], [-1, 8], [0, 8]], 8, 0)
+    resets(V("rst8"), 8)
+    ms(V("b0"), 0.0)
+    ts(V("si", 2, 3), col("si", 0), 15, A.bitwise_and)
+    ts(V("si", 3, 4), col("si", 0), 7, A.bitwise_and)
+    ts(V("si", 4, 5), col("si", 0), 3, A.logical_shift_right, 1, A.bitwise_and)
+    ts(V("si", 5, 6), col("si", 0), 4, A.logical_shift_right, 1, A.bitwise_and)
+    ts(V("si", 6, 7), col("si", 0), 3, A.bitwise_and)
+    ms(V("d12"), 1.0)
+    cp(V("pv", 0, 5), V("si", 2, 7))
+    ts(col("pv", 5), col("si", 5), -1.0, A.mult, 1.0, A.add)
+    ts(col("pv", 8), col("si", 2), 15.0, A.is_lt, 2.0, A.mult)
+    ms(V("et"), 0.0)
+    rows = paint(PLACES + PAIRS)
+    some(rows, 6)
+    act(col("pv", 6), col("pv", 0), 32.0)
+    lin(col("pv", 11), col("pv", 4), 16.0, 15.0)
+    ts(V("s16", 32, 48), V("s16", 0, 16), col("pv", 0), A.is_equal, -4096.0, A.mult)
+    ts(V("s16", 16, 32), V("s16", 16, 32), col("pv", 0), A.is_equal, 1024.0, A.mult)
+    ts(V("rep"), V("ones", 0, 32), col("pv", 0), A.mult)
+    tt(V("s16", 16, 32), V("s16", 16, 32), V("s16", 32, 48), A.add)
+    for v in range(2):
+        for e in range(2):
+            ts(V("t64", 32 * v + 16 * e, 32 * v + 16 * e + 16), V("pi", v, 32, 2), col("pv", 5 - 2 * e), A.mult)
+    ts(V("fast"), V("q8"), col("pv", 1), A.add)
+    trans(V("u64"), V("t64"))
+    cp(V("ul"), V("ia", 0, 8))
+    for v in range(2):
+        tt(V("opf", 16 * v, 16 * v + 16), V("u64", 32 * v, 32 * v + 16), V("u64", 32 * v + 16, 32 * v + 32), A.add)
+    ts(V("wd"), V("opf"), col("pv", 6), A.subtract)
+    if not all(roles):
+        gaps()
+    some(rows, ROWS_EARLY)
+    act(V("selk"), I(V("s16", 16, 32), V("rep")))
+    quant("u", V("ut"), 0, 128)
+    ready = preparing(0)
+    some(ready, 4 if roles[0] else 2)
+    call("v", [V("qu2")], [I(V("qu"), V("ul"))], lambda: g.vector.tensor_copy(ap(V("qu2"), dt.uint32), ap(I(V("qu"), V("ul")), dt.uint32)))
+    call("s", [V("su2")], [I(V("su"), V("ul"))], lambda: g.scalar.activation(ap(V("su2")), ap(I(V("su"), V("ul"))), AF.Copy))
+    act(V("sel2"), V("selk", 0, 256), 2.0 ** -9)
+    some(ready, 3)
+    early(0)
+    cp(V("al"), V("opf", 0, 32, 2))
+    weights = fixed()
+    some(weights, FIXED_EARLY)
+    cp(V("bl"), V("opf", 1, 32, 2))
+    weave(rows)
+    lists = tables()
+    ts(V("sgl"), V("q8", 0, 16, 2), 8.0, A.mult, col("pv", 11), A.add)
     if roles[0]:
         ts(V("dd", 16, 32), V("dd", 0, 16), -1.0, A.mult)
-    for k in range(2):
-        quant("x", V("x0", 1024 * k, 1024 * k + 1024), 256 * k, 256 * k + 256)
-        act(V("ssb", 256 * k, 256 * k + 256), mm(k, mx("u2", 0, 128), mx("x", 256 * k, 256 * k + 256)))
-    for b in range(4):
-        ts(V("h0", 32 * b, 32 * b + 32), V("hi"), 4.0, A.mult, float(b), A.add)
-    ms(V("rst8"), 1.0)
-    cp(V("lists", 0, 48), V("stg", 0, 48))
-    ms(V("rst8", 0, 256, 8), 0.0)
+    for k, (a, e) in enumerate(X0):
+        quant("x", V("x0", 4 * a, 4 * e), a, e)
+        if k == 0:
+            scan(V("vecs"), V("selk", 0, 192), V("rows"), A.add, A.max)
+            some(lists, LISTS_EARLY)
+            weave(ready)
+        o = mm(k, mx("u2", 0, 128), mx("x", a, e))
+        if e == C:
+            cp(V("hn"), V("hi"))
+            for b in range(4):
+                ts(V("h0", 32 * b, 32 * b + 32), V("hi"), 4.0, A.mult, float(b), A.add)
+        move("v" if e == C else "s", V("ssb", a, e), o)
     xcur = "x0"
     for r, step in enumerate(STEPS):
         peer = T.cores[rank ^ step]
         left = roles[r]
         last = r == len(STEPS) - 1
-        snd, lnd = "snd%d" % r, V("lnd%d" % r)
+        snd, lnd, ahead = "snd%d" % r, V("lnd%d" % r, 0, 32), V("lnd%d" % r, 32, 64)
 
         def by_letter(b):
             act(V("xl", 512 * b, 512 * b + 512), I(V(xcur), V("h1l" if r else "h0", 32 * b, 32 * b + 32)))
@@ -359,159 +375,187 @@ def rank_program(g, core, T, topo):
             act(V(src, 0, 256), I(V("ssb"), V("hn", 0, 16)))
             cp(V(src, 256, 512), I(V("ssb"), V("hn", 16, 32)))
         act(V("bs", 128, 256), I(V(src), V("bl", 8, 16)))
+        if r == 1:
+            tt(V("hf"), V("hf"), V("ib"), A.add)
+            for b in range(4):
+                lin(V("h4b", 32 * b, 32 * b + 32), V("hf"), 4.0, float(b))
+        elif r == 0:
+            if not all(roles):
+                lin(V("kback"), V("kback"), 1.0, col("base", 3))
+            some(lists, LISTS_NEXT)
+        if r and left:
+            act(V("ob"), I(ahead, V("il", 0, 13)))
+        if r > 1:
+            by_letter(0)
         cp(V("bs", 0, 128), I(V(src), V("bl", 0, 8)))
-        for k in range(2):
-            tt(V("fl", 128 * k, 128 * k + 128), I(V(src), V("al", 8 * k, 8 * k + 8)), V("bs", 128 * k, 128 * k + 128), A.is_lt)
+        tt(V("fl"), I(V(src), V("al")), V("bs"), A.is_lt)
+        if r == 1:
+            cp(V("h1l"), V("h4b"))
+            by_letter(0)
         scan(V("fsc"), V("sel2"), V("fl"), A.add, A.max)
         flags = V("fsc", 15, 256, 16)
-        mine = "r0" if r == 0 else snd
-        word = mine if left else "df"
+        mine = snd if left and r else "r0"
         if left and r == 0:
             tt(V(snd, 0, 32, 2), flags, V("dd", 0, 16), A.mult)
             tt(V(snd, 1, 32, 2), flags, V("dd", 16, 32), A.mult)
-        else:
-            if not left:
-                tt(V("sg1"), I(V("fsc"), V("sgl")), V("sig"), A.mult)
+        elif left:
             tt(V("tt"), flags, V("dd", 0, 16), A.mult)
-            if not left:
-                scan(V("sg2"), V("rst4"), V("sg1"), A.mult, A.add)
-            tt(V(word, 0, 32, 2), V("w0", 0, 32, 2), V("tt"), A.add)
-            if not left and r == 0:
-                cp(V(snd), V("sg2", 3, 128, 4))
-            elif not left:
-                tt(V(snd), V("r0"), V("sg2", 3, 128, 4), A.add)
-            tt(V(word, 1, 32, 2), V("w0", 1, 32, 2), V("tt"), A.subtract)
-        send(peer, lnd, V(snd), "a%d" % (3 * r))
-        if r == 0:
-            for b in range(4):
-                e = V("et", 512 * b, 512 * b + 512)
-                call("g", [e], [V("six")], lambda: g.affine_select(ap(e), ap(V("six")), [[-1, 512]], A.is_equal, 0.0, b, 4))
-            if roles[0] and not all(roles):
-                iota(V("tslow"), [[8, 4], [1, 8], [0, 8]], 0, 0)
-                iota(V("tfast"), [[8, 4], [0, 8], [1, 8]], 0, 0)
-            rank_tables()
-            fixed()
-            tt(V(mine), V("v0"), V(snd), A.add)
-            cp(V("lists", 48, 128), V("stg", 48, 128))
-            cp(V("o1"), I(V(mine), V("il", 0, 13)))
+            tt(V(snd, 0, 32, 2), V("w0", 0, 32, 2), V("tt"), A.add)
+            tt(V(snd, 1, 32, 2), V("w0", 1, 32, 2), V("tt"), A.subtract)
         else:
-            by_letter(0)
-            act(V("o1"), I(V(mine), V("il", 0, 13)))
+            tt(V("sg1"), I(V("fsc"), V("sgl")), V("sig"), A.mult)
+            scan(V("sg2"), V("rst4"), V("sg1"), A.mult, A.add)
+            cp(V(snd, 0, 32), V("sg2", 3, 128, 4))
+            tt(V(mine), V("sg2", 3, 128, 4), V("rsc", 7, 256, 8), A.add)
+        send(peer, lnd, V(snd, 0, 32), "a%d" % (3 * r))
+        if r == 0:
+            dma("y", ap(V("qw"), dt.uint8), T.wc[:], [V("qw")], [lnd])
+            dma("y", ap(V("sw")), T.ws[:], [V("sw")], [])
+            dma("y", ap(V("vt")), T.v[:], [V("vt")], [])
+            weave(weights)
+            iota(V("itab"), [[0, 4], [1, 8]], 0, 0)
+            if left:
+                iota(V("kslow"), [[0, 4], [1, 8], [0, 8]], 0, 0)
+            iota(V("iota"), [[1, 512]], 0, 0)
+            cp(V("lists", 0, 32), V("stg", 0, 32))
+            if left:
+                tt(V(mine), V(snd, 32, 64), V(snd, 0, 32), A.add)
+            iota(V("erow", 0, NT), [[0, NT]], 0, 0)
+            iota(V("place"), [[1, 16], [16, 32]], 0, 0)
+            select(V("et"), V("et"), [[-1, 528]], A.not_equal, 16.0, 3, 4)
+            if left and not all(roles):
+                iota(V("tslow"), [[8, 4], [1, 8], [0, 8]], 0, 0)
+            if not left and any(roles):
+                iota(V("kslow"), [[0, 4], [1, 8], [0, 8]], 0, 0)
+        sign = -1.0 if left else 1.0
+        act(V("m64"), V(mine, 0, 32), -64.0 * sign)
+        lin(V("o1"), I(V(mine, 0, 32), V("il", 0, 13)), 64.0 * sign, 32.0 * sign)
+        if left and r == 0:
+            act(V("ob"), I(ahead, V("il", 0, 13)))
+        if r == 0:
+            weave(lists)
         if left:
             tt(V("df", 0, 31), V(mine, 0, 31), V(mine, 1, 32), A.subtract)
+            if r:
+                tt(V("x1"), I(ahead, V("kl", 0, 13)), V("ob"), A.subtract)
             cp(V("df", 7, 32, 8), V(mine, 7, 32, 8))
         else:
-            tt(V("dtl"), I(V(word), V("slow")), V("tfast"), A.is_equal)
-        tt(V("own"), I(V(mine), V("kl", 0, 13)), V("o1"), A.is_le)
+            tt(V("dtl"), I(V(mine, 0, 32), V("fast")), V("kback"), A.is_equal)
         if r == 0:
             ms(V("mlt", 0, 16), 0.0)
-        ts(V("own"), V("own"), -64.0, A.mult)
-        if r == 0:
             ts(V("mlt", 16, 32), V("s16", 0, 16), col("pv", 0), A.is_lt)
-            tt(V("lv1"), V("lv0"), lnd, A.add)
-            lnd = V("lv1")
-            if not all(roles):
-                ts(V("rneg8"), V("rst8"), 128.0, A.mult, -128.0, A.add)
+        tt(V("own"), I(V("m64"), V("kl", 0, 13)), V("o1"), A.add)
+        if r == 0:
+            cp(V("lists", 32, 112), V("stg", 32, 112))
+            if left:
+                tt(V("x1"), I(ahead, V("kl", 0, 13)), V("ob"), A.subtract)
+            else:
+                tt(V("lv1"), ahead, lnd, A.add)
+                lnd = V("lv1")
             by_letter(0)
         if left:
+            tt(V("x1"), V("x1"), V("own"), A.min)
             act(V("dtl"), I(V("df"), V("fast")))
         else:
             for q in range(4):
                 lin(V("dtl", 64 * q, 64 * q + 64), V("dtl", 64 * q, 64 * q + 64), 64.0, 8.0 * q - 64.0)
-        for b in range(1, 4):
+        if r == 0:
+            lin(col("tabd", 32), col("pv", 6), 1.0, 511.0)
+            lin(col("tabd", 33), col("pv", 6), 1.0, 543.0)
+            lin(V("tabd", 0, 32), V("i64", 2, 34), 1.0, col("tabd", 32))
+            act(col("pv", 7), col("pv", 8), 512.0)
+        for b in range(1, 3 if r else 2):
             by_letter(b)
-        if r == 0:
-            lin(V("tabd"), V("iota", 0, 32), 1.0, col("pv", 14))
-            lin(V("tabn"), V("iota", 0, 32), 16.0, col("pv", 0))
-            act(V("erow", 0, NT), V("ones", 0, NT), 0.0)
-        tt(V("x1", 0, 64), I(lnd, V("il", 0, 4)), V("own", 0, 64), A.subtract)
-        tt(V("x1", 64, 208), I(lnd, V("il", 4, 13)), V("own", 64, 208), A.subtract)
-        tt(V("b0", 0, 128, 2), I(lnd, V("kl", 0, 4)), V("x1", 0, 64), A.is_le)
-        tt(V("lg", 0, 64), I(lnd, V("kl", 4, 8)), V("x1", 64, 128), A.is_le)
-        scan(V("w", 128, 240), V("b0", 0, 112), V("b0", 16, 128), A.mult, A.max)
-        tt(V("d12", 8, 256, 16), I(lnd, V("kl", 12, 13)), V("x1", 192, 208), A.is_le)
-        tt(V("pp", 0, 64), I(V("w", 0, 256), V("gl", 0, 4)), V("lg", 0, 64), A.mult)
-        tt(V("lg", 64, 128), I(lnd, V("kl", 8, 12)), V("x1", 128, 192), A.is_le)
-        scan(V("w", 256, 384, 2), V("d12", 0, 64), V("pp", 0, 64), A.mult, A.max)
-        if r:
-            act(V("wi", 64, 256), I(V("w", 0, 384), V("rki", 4, 16)))
-        tt(V("pp", 64, 128), I(V("w", 0, 384), V("gl", 4, 8)), V("lg", 64, 128), A.mult)
-        if r == 0:
-            cp(V("wi", 64, 256), I(V("w", 0, 384), V("rki", 4, 16)))
-        scan(V("w", 384, 512, 2), V("d12", 64, 128), V("pp", 64, 128), A.mult, A.max)
-        cp(V("wi", 0, 64), I(V("w"), V("rki", 0, 4)))
-        tt(V("cmp", 64, 256), I(V("w"), V("rkk", 4, 16)), V("wi", 64, 256), A.is_gt)
-        tt(V("cmp", 0, 64), I(V("w"), V("rkk", 0, 4)), V("wi", 0, 64), A.is_gt)
-        scan(V("pos"), V("rst8"), V("cmp"), A.mult, A.add)
-        if left:
-            tt(V("ne"), I(V("pos"), V("posl")), V("kslow"), A.not_equal)
-        else:
-            tt(V("ne"), I(V("pos"), V("posl")), V("dtl"), A.add)
-        tt(V("mv"), I(V("pos"), V("mvl")), V("itab"), A.not_equal)
-        if left:
-            scan(V("nw"), V("ne"), V("dtl"), A.mult, A.add)
-        else:
-            scan(V("nw"), V("rneg8"), V("ne"), A.add, A.max)
-        scan(V("cc"), V("onef"), V("mv"), A.mult, A.add)
-        ts(V("zl"), V("nw", 7, 256, 8), col("pv", 6), A.add)
 
-        for k in range(2):
-            for b in range(4):
-                act(V("z", 1024 * k + b, 1024 * k + 1024, 4), I(V("xl", 512 * b, 512 * b + 512), V("zl", 16 * k, 16 * k + 16)))
-        cp(V("tot"), V("cc", 30, 32))
-        ts(V("h1"), V("mv"), -2048.0, A.mult, 2047.0, A.add)
-        tt(V("tr"), I(V("iota", 0, 64), V("tot")), V("mlt"), A.mult)
-        tt(V("h1"), V("h1"), V("cc"), A.add)
-        call("v", [col("base", 0)], [V("tr")], lambda: g.vector.tensor_reduce(ap(col("base", 0)), ap(V("tr")), AxisListType.X, A.add))
-        tt(V("h1"), V("h1"), V("tabd"), A.min)
-        cp(V("wd"), V("nw", 7, 256, 8))
-        ts(V("dst"), V("h1"), col("base", 0), A.add)
-        cp(I(V("erow"), V("dst")), V("iota"))
+        def leads(o, a, e):
+            tt(o, I(lnd, V("il" if left else "kl", a, e)), V("x1", 16 * a, 16 * e), A.is_ge if left else A.is_le)
+
+        if not left:
+            tt(V("x1", 0, 64), I(lnd, V("il", 0, 4)), V("own", 0, 64), A.max)
+            tt(V("x1", 64, 208), I(lnd, V("il", 4, 13)), V("own", 64, 208), A.max)
+        leads(V("b0", 16, 144, 2), 0, 4)
+        leads(V("lg", 0, 64), 4, 8)
+        scan(V("w", W7, 240), V("b0", 15, 128), V("b0", 31, 144), A.mult, A.max)
+        leads(V("d12", 2, 130, 8), 12, 13)
+        act(V("w", YES, 512, 32), V("d12", 74, 129, 16), HUGE)
+        lin(V("w", NO, 512, 32), V("d12", 74, 129, 16), -HUGE, HUGE)
+        tt(V("pp", 0, 64), I(V("w", 0, 256), V("gl", 0, 4)), V("lg", 0, 64), A.mult)
+        leads(V("lg", 64, 128), 8, 12)
+        scan(V("w", 256, 384, 2), V("d12", 0, 64), V("pp", 0, 64), A.mult, A.max)
+        act(V("wi", 192, 256), I(V("w", 0, 512), V("soon", 12, 16)))
+        act(V("wi", 0, 192), I(V("w", 0, 512), V("soon", 0, 12)))
+        for b in range(3 if r else 2, 4):
+            by_letter(b)
+        tt(V("pp", 64, 128), I(V("w", 0, 384), V("gl", 4, 8)), V("lg", 64, 128), A.mult)
+        scan(V("w", 512, 640, 2), V("d12", 65, 129), V("pp", 64, 128), A.mult, A.max)
+        tt(V("cmp", 192, 256), I(V("w"), V("late", 12, 16)), V("wi", 192, 256), A.is_lt)
+        tt(V("cmp", 0, 192), I(V("w"), V("late", 0, 12)), V("wi", 0, 192), A.is_gt)
+        scan(V("pos"), V("rst8"), V("cmp"), A.mult, A.add)
+
         outs = {}
-        for what, k, b in LPLAN:
-            piece = V("z32", 512 * b + 256 * k, 512 * b + 256 * k + 256)
-            if what == "q":
+        steps = {
+            "mv": lambda: tt(V("mv"), I(V("pos"), V("mvl")), V("itab"), A.not_equal),
+            "cc": lambda: scan(V("cc"), V("ones", 0, 32), V("mv"), A.add, A.add, col("tabd", 32)),
+            "ha": lambda: tt(V("h1"), V("mv"), V("tabd", 0, 32), A.mult),
+            "hb": lambda: tt(V("h1"), V("cc"), V("h1"), A.subtract),
+            "tot": lambda: ts(V("tot"), V("cc", 30, 32), col("tabd", 33), A.subtract),
+            "tr": lambda: tt(V("tr"), I(V("i64"), V("tot")), V("mlt"), A.mult),
+            "base": lambda: call("v", [col("base", 0)], [V("tr")], lambda: g.vector.tensor_reduce(ap(col("base", 0)), ap(V("tr")), AxisListType.X, A.add)),
+            "dst": lambda: ts(V("dst"), V("h1"), col("base", 0), A.add),
+            "sc": lambda: cp(I(V("erow"), V("dst")), V("iota")),
+            "esc": lambda: scan(V("esc"), V("selk", 0, NT), V("erow", 0, NT), A.add, A.max),
+            "el": lambda: ts(V("el"), V("esc", 15, NT, 16), col("pv", 7), A.subtract),
+        }
+        for w in LPLAN:
+            if w in steps:
+                steps[w]()
+            elif w[:2] in ("ne", "nw", "zl"):
+                k = int(w[2])
+                ne, nw, dtl, kslow, rst8 = [V(n, 128 * k, 128 * k + 128) for n in ("ne", "nw", "dtl", "kslow", "rst8")]
+                if w[:2] == "ne":
+                    tt(ne, I(V("pos"), V("posl", 8 * k, 8 * k + 8)), kslow if left else dtl, A.not_equal if left else A.add)
+                elif w[:2] == "nw":
+                    scan(nw, ne if left else rst8, dtl if left else ne, A.mult, A.add if left else A.max)
+                else:
+                    ts(V("zl", 16 * k, 16 * k + 16), V("nw", 128 * k + 7, 128 * k + 128, 8), col("pv", 6), A.add)
+            elif w[0] == "q":
+                k = int(w[1])
                 quant("z", V("z", 1024 * k, 1024 * k + 1024), 256 * k, 256 * k + 256)
                 outs[k] = [mm(4 * k + n, mx("w", 128 * n, 128 * n + 128), mx("z", 256 * k, 256 * k + 256)) for n in range(4)]
-            elif what in "zs":
-                move("v" if what == "z" else "s", piece, V("z", 1024 * k + b, 1024 * k + 1024, 4), 32.0)
-            elif what == "a":
-                tt(V("yg", YW * b + 256 * k, YW * b + 256 * k + 256), outs[k][b], piece, A.add)
-            elif what == "e":
-                scan(V("esc"), V("selk", 0, NT), V("erow", 0, NT), A.add, A.max)
+            elif w[0] == "f":
+                b, c0, c1 = int(w[2]), int(w[3], 16), int(w[4], 16)
+                move(w[1], V("ft", 64 * c0 + b, 64 * c1, 4), I(V("yg", YW * b, YW * b + C), V("el", c0, c1)), 2.0 ** -5)
             else:
-                ts(V("el"), V("esc", 15, NT, 16), col("pv", 7), A.subtract)
-        for q, b, c0, c1 in FPLAN:
-            move(q, V("ft", 64 * c0 + b, 64 * c1, 4), I(V("yg", YW * b, YW * b + C), V("el", c0, c1)), 2.0 ** -5)
-        if r == 0:
-            ts(V("ia"), V("hi"), 31, A.bitwise_and)
-            ts(V("ib"), V("hi"), 5, A.logical_shift_right)
+                k, b = int(w[-2]), int(w[-1])
+                z, z32 = V("z", 1024 * k + b, 1024 * k + 1024, 4), V("z32", 512 * b + 256 * k, 512 * b + 256 * k + 256)
+                if w[0] == "g":
+                    move(w[1], z, I(V("xl", 512 * b, 512 * b + 512), V("zl", 16 * k, 16 * k + 16)))
+                elif w[0] == "z":
+                    move(w[1], z32, z, 32.0)
+                else:
+                    tt(V("yg", YW * b + 256 * k, YW * b + 256 * k + 256), outs[k][b], z32, A.add)
         quant("f%d" % r, V("ft"), 0, NT)
         send(peer, V("lq%d" % r), V("qf%d" % r), "a%d" % (3 * r + 1), dt.uint8)
         send(peer, V("ls%d" % r), V("sf%d" % r), "a%d" % (3 * r + 2))
         if r == 0:
-            ts(V("hf"), V("ia"), 16.0, A.mult)
-            act(V("f16"), V("ft"), 16.0)
-            tt(V("hf"), V("hf"), V("ib"), A.add)
-            cp(V("hp"), V("hf"))
-            act(V("hrow"), I(V("iota"), V("hp")))
-            quant("e", V("et"), 0, 512)
+            lin(V("tabn"), V("i64", 0, 32), 16.0, col("pv", 0))
+            act(V("hrow"), I(V("place"), V("hn")))
+            for b in range(4):
+                quant("e", V("et", 3 - b, 515 - b), 128 * b, 128 * b + 128)
+        later = state_list()
+        next(later)
         if not last:
             act(V("hw"), I(V("hrow"), V("zl")))
-        if r:
-            act(V("f16"), V("ft"), 16.0)
+        act(V("f16"), V("ft"), 16.0)
         if not last:
-            weave(state_list(), preparing(roles[r + 1]))
+            weave(preparing(r + 1), later)
             cp(V("xll"), V("h4"))
-            if r == 0:
-                for b in range(4):
-                    ts(V("h1l", 32 * b, 32 * b + 32), V("hf"), 4.0, A.mult, float(b), A.add)
             scan(V("hsc"), V("selk"), V("hw"), A.add, A.max)
         else:
-            weave(state_list())
+            weave(later)
             for v in range(2):
                 for e in range(2):
-                    ts(V("t64", 32 * v + 16 * e, 32 * v + 16 * e + 16), V("h4", 16 * v, 16 * v + 16), col("pv", 4 + e), A.mult)
+                    ts(V("t64", 32 * v + 16 * e, 32 * v + 16 * e + 16), V("h4", 16 * v, 16 * v + 16), col("pv", 5 - 2 * e), A.mult)
             ts(V("opf"), V("wd"), col("pv", 6), A.add)
             trans(V("u64"), V("t64"))
             quant("v", V("vt"), 0, 128)
@@ -525,9 +569,12 @@ def rank_program(g, core, T, topo):
                 ts(V("al"), V("hsc", 15, 512, 32), col("pv", 7), A.subtract)
                 ts(V("bl"), V("hsc", 31, 512, 32), col("pv", 7), A.subtract)
             tt(V("yg", YW * b + C, YW * b + YW), o, V("f16", b, 4 * NT, 4), A.add)
+        if not last:
+            order("g", [], [V("ls%d" % r)], ("sent", 0))
+            early(r + 1)
         xcur = "xa"
         bank, after = 0, []
-        for q, a, e, b in XPLAN:
+        for q, a, e, b in XLAST if last else XPLAN:
             if q != "q":
                 move(q, V(xcur, 4 * a + b, 4 * e, 4), I(V("yg", YW * b, YW * b + YW), V("xll", a // 16, e // 16)), 2.0 ** -5)
                 continue
@@ -536,12 +583,17 @@ def rank_program(g, core, T, topo):
                 dma("y", T.oc[:, 4 * a:4 * e], ap(V("qx", a, e), dt.uint8), [], [V("qx", a, e)])
             after.append((a, e, b, mm(bank, mx("v" if last else "u2", 0, 128), mx("x", a, e))))
             bank += 1
+        if r == 0:
+            ts(V("ia"), V("hi"), 31, A.bitwise_and)
+            ts(V("ib"), V("hi"), 5, A.logical_shift_right)
+            ts(V("hf"), V("ia"), 16.0, A.mult)
         for a, e, q, o in after:
+            if last and e == C:
+                for k in range(4):
+                    dma("ys"[k % 2], T.osc[4 * k:4 * k + 4, :], T.sx[32 * k:32 * k + 4, :], [], [V("sx")])
             move(q, V("yo" if last else "ssb", a, e), o)
             if last:
                 dma("s", T.y[:, a:e], ap(V("yo", a, e)), [], [V("yo", a, e)])
 
-    for k in range(4):
-        dma("y", T.osc[4 * k:4 * k + 4, :], T.sx[32 * k:32 * k + 4, :], [], [V("sx")])
-    for s in sorted(total):
+    for s in sorted(total, key=lambda s: int(s[1:]) if s[0] == "d" else -1):
         wait("g", (s, total[s]))

from concourse.mybir import dt, AluOpType as A, AxisListType, ActivationFunctionType as AF

C, NT, STEPS = 512, 224, [1, 2, 3]
YW = C + NT
CODE = "float8_e4m3fn_x4"
SCRATCH = {}
POOL, _at = {}, [0]


def _buf(name, n, dtype, where="sbuf"):
    SCRATCH[name] = (where, [128, n], dtype)


for _n, _w in [("x0", 2048), ("xa", 2048), ("xl", 2048), ("z", 2048), ("z32", 2048), ("yg", 4 * YW), ("ft", 4 * NT), ("f16", 4 * NT), ("ut", 512), ("vt", 512),
               ("et", 528), ("fl", 256), ("fsc", 256), ("sel2", 256), ("w", 640), ("b0", 144), ("lg", 128), ("d12", 256), ("pp", 128), ("x1", 208),
               ("o1", 208), ("own", 208), ("ob", 208), ("gap", 256), ("turn", 256), ("far", 256), ("wi", 256), ("cmp", 256), ("pos", 256), ("ne", 256), ("nw", 256),
               ("dtl", 256), ("kslow", 256), ("kback", 256), ("tslow", 256), ("rst8", 256), ("rst4", 128), ("ones", 256), ("sig", 128), ("sg1", 128), ("sg2", 128),
               ("nei", 256), ("rsc", 256), ("wd", 32), ("w0", 32), ("r0", 32), ("df", 32), ("dd", 32), ("m64", 32), ("lv1", 32), ("tt", 16), ("itab", 32)]:
    _buf(_n, _w, "bfloat16")
for _r in range(3):
    _buf("snd%d" % _r, 64, "bfloat16"); _buf("lnd%d" % _r, 64, "bfloat16")
    _buf("qf%d" % _r, NT, CODE); _buf("sf%d" % _r, NT, "uint8"); _buf("lq%d" % _r, NT, CODE); _buf("ls%d" % _r, NT, "uint8")
for _n, _w in [("qx", 512), ("qz", 512), ("qw", 512), ("qe", 512), ("qu", 128), ("qu2", 128), ("qv", 128)]:
    _buf(_n, _w, CODE); _buf("s" + _n[1:], _w, "uint8")
for _n, _w in [("ssb", 512), ("bs", 256), ("iota", 512), ("place", 512), ("selk", 512), ("erow", 2048), ("esc", NT), ("hrow", 512), ("hw", 512), ("hsc", 512), ("yo", 512),
               ("pv", 16), ("s16", 48), ("rows", 192), ("stg", 128), ("vecs", 192), ("h4b", 128), ("q8", 16), ("c2", 16), ("i64", 64),
               ("t64", 64), ("u64", 64), ("mv", 32), ("cc", 32), ("h1", 32), ("h3", 32), ("h4", 32), ("tabn", 32), ("tabd", 34), ("vc", 12), ("mlt", 32), ("tr", 32),
               ("base", 4), ("opf", 32), ("hf", 32), ("qk", 16)]:
    _buf(_n, _w, "float32")
for _n, _w in [("pi", 32), ("hi", 32), ("ia", 32), ("ib", 32), ("si", 8)]:
    _buf(_n, _w, "int32")
for _n, _w in [("il", 14), ("kl", 14), ("gl", 8), ("late", 16), ("soon", 16), ("posl", 16), ("mvl", 2), ("pad", 16), ("fast", 16), ("sgl", 8), ("rep", 32),
               ("h0", 128), ("h1l", 128), ("hn", 32), ("zl", 32), ("al", 16), ("bl", 16), ("tot", 2), ("dst", 32), ("el", 14), ("xll", 32)]:
    POOL[_n] = ("lists", _at[0], _w)
    _at[0] += -(-_w // 16) * 16
_buf("lists", _at[0], "uint16")
_buf("ul", 8, "uint16")
_buf("ps", 4096, "float32", "psum")
SEMAPHORES = ["qv", "qs", "qt", "qg", "sent"] + ["d%d" % i for i in range(24)] + ["a%d" % i for i in range(12)]

F = [1.25, 1.5, 2.0, 4.0, 16.0, 256.0, 2.0 ** 16, 2.0 ** 32]
B3, B2, B1, B0 = 1, 2, 3, 4
W7, W6, W5, W4A, NIL, W4B = 127, 129, 131, 133, 135, 139
W4, W3, W2, YES, NO, W1, W0, HUGE = 258, 272, 286, 385, 386, 526, 542, 2.0 ** 40
PAIRS = [(34, 42, 1, 3, 0), (42, 48, 1, 2, 0), (50, 53, 1, 7, -1), (58, 62, 1, 7, -1), (62, 63, 1, 4, 0), (56, 64, 7, 3, -1),
         (64, 72, 1, 1, 0), (81, 88, 1, 7, -1), (89, 95, 1, 7, -1), (5, 16, 8, 4, 0), (24, 32, 1, 7, 0)]
PLACES = [(129, 132, 1, W7, 2), (132, 135, 1, W4, 14), (122, 126, 1, W7, 2), (114, 117, 1, W7, 2), (136, 144), (112, 128, 14, W4B, 0), (113, 114, 1, W4A, 0), (144, 160),
          (120, 128, 7, B3, 1), (160, 192), (135, 144, 8, B1, 1), (144, 160, 8, W1, 0), (151, 160, 8, W0, 0), (167, 176, 8, YES, 0), (176, 192, 8, NO, 0)]
X0 = [(0, 384), (384, 512)]
ROWS_EARLY, FIXED_EARLY, LISTS_EARLY, LISTS_NEXT = 20, 17, 4, 22
LPLAN = ("ne0 mv nw0 cc zl0 gs00 gs01 gs02 gs03 ha tot ne1 tr hb nw1 base zl1 gs10 gs11 gs12 gs13 dst zv00 sc q0 esc zv03 zv02 el q1 "
         "zs01 zs10 zs11 zs12 zs13 a00 a01 a10 a11 a02 a12 a03 a13 fs00e fs10e fs20e fv308 fs38e").split()


def _pieces(cuts, plan):
    return [(w[0], cuts[int(w[1])], cuts[int(w[1]) + 1], w[2] if w[0] == "q" else int(w[2])) for w in plan.split()]


XPLAN = _pieces((0, 192, 384, 512), "s00 s01 s02 v12 v03 s10 s11 v13 q0s s21 s20 v23 v22 q1s q2v")
XLAST = _pieces((0, 288, 512), "s00 s01 s02 v03 s10 s11 v13 q0s v12 q1v")


def rank_program(g, core, T, topo):
    rank = T.rank_of(core)
    if rank is None:
        return
    Q = {"v": g.vector, "s": g.scalar, "t": g.tensor, "g": g, "y": g.sync}
    count = {"v": 0, "s": 0, "t": 0, "g": 0}
    seen = {q: {} for q in Q}
    total = {}
    log = {}
    nd = [0]

    def V(name, a=0, b=None, s=1):
        if name in POOL:
            pool, at, n = POOL[name]
            return (pool, at + a, at + (n if b is None else b), s)
        return (name, a, SCRATCH[name][1][1] if b is None else b, s)

    def S(name, a=0, b=None, s=1):
        return ("stg",) + V(name, a, b, s)[1:]

    def I(win, off):
        return ("ind", win, off)

    def ap(v, cast=None):
        if not isinstance(v, tuple):
            return v
        if v[0] == "ind":
            return ap(v[1], cast).indirect(ap(v[2]))
        a = T[v[0]][:, v[1]:v[2]:v[3]] if v[3] != 1 else T[v[0]][:, v[1]:v[2]]
        return a.bitcast(cast) if cast is not None else a

    def cols(v):
        if v[0] == "ps":
            return set(range(v[1] // 512, (v[2] - 1) // 512 + 1))
        return set(range(v[1], v[2], v[3]))

    def wait(q, tok):
        if seen[q].get(tok[0], 0) < tok[1]:
            Q[q].wait_ge(T.sem[tok[0]], tok[1])
            seen[q][tok[0]] = tok[1]

    def order(q, outs, ins, tok):
        rd, wr = [], []
        for v in ins:
            if isinstance(v, tuple):
                rd += [v[1], v[2]] if v[0] == "ind" else [v]
        for v in outs:
            if v[0] == "ind":
                wr.append(v[1]); rd.append(v[2])
            else:
                wr.append(v)
        need = {}
        for vs, w in ((rd, False), (wr, True)):
            for v in vs:
                cs = cols(v)
                for e in log.setdefault(v[0], []):
                    if (e[1] or w or (v[0] == "ps" and e[2][0] != "q" + q)) and cs & e[0]:
                        need[e[2][0]] = max(need.get(e[2][0], 0), e[2][1])
        for s in sorted(need):
            wait(q, (s, need[s]))
        for v in wr:
            cs = cols(v)
            log[v[0]] = [e for e in log[v[0]] if not e[0] <= cs] + [(cs, True, tok)]
        for v in rd:
            log[v[0]].append((cols(v), False, tok))

    def call(q, outs, ins, make):
        count[q] += 1
        tok = ("q" + q, count[q])
        order(q, outs, ins, tok)
        make().then_inc(T.sem["q" + q], 1)
        total["q" + q] = count[q]

    def dma(q, out, in_, outs, ins):
        tok = ("d%d" % nd[0], 16)
        nd[0] += 1
        order(q, outs, ins, tok)
        Q[q].dma_start(out, in_).then_inc(T.sem[tok[0]], 16)
        total[tok[0]] = 16

    def send(peer, dst, src, sem, cast=None, writes=True, gets=True):
        if writes:
            rid, pid, _e = topo.addr(peer)
            total["sent"] = total.get("sent", 0) + len(topo.engines(core, peer))
            order("g", [], [src], ("sent", 0))
            g.remote_dma(ap(dst, cast), ap(src, cast), T.sem[sem], T.sem.sent, pid, rid, topo.mask(core, peer))
        if gets:
            total[sem] = len(topo.engines(peer, core))
            log.setdefault(dst[0], []).append((cols(dst), True, (sem, total[sem])))

    def cp(o, i): call("v", [o], [i], lambda: g.vector.tensor_copy(ap(o), ap(i)))
    def tt(o, a, b, op): call("v", [o], [a, b], lambda: g.vector.tensor_tensor(ap(o), ap(a), ap(b), op))
    def ts(o, a, s1, op, s2=None, op1=None):
        if op1 is None:
            call("v", [o], [a, s1], lambda: g.vector.tensor_scalar(ap(o), ap(a), ap(s1), None, op))
        else:
            call("v", [o], [a, s1, s2], lambda: g.vector.tensor_scalar(ap(o), ap(a), ap(s1), ap(s2), op, op1))
    def scan(o, a, b, op0, op1, first=0.0): call("v", [o], [a, b, first], lambda: g.vector.tensor_tensor_scan(ap(o), ap(a), ap(b), ap(first), op0, op1))
    def ms(o, c): call("v", [o], [], lambda: g.vector.memset(ap(o), c))
    def act(o, i, c=1.0): call("s", [o], [i], lambda: g.scalar.activation(ap(o), ap(i), AF.Copy, scale=float(c)))
    def lin(o, i, c, b): call("s", [o], [i, b], lambda: g.scalar.activation(ap(o), ap(i), AF.Identity, bias=ap(b), scale=float(c)))
    def move(q, o, i, c=1.0):
        if q == "s":
            act(o, i, c)
        elif c == 1.0:
            cp(o, i)
        else:
            ts(o, i, float(c), A.mult)
    def quant(q, t, a, b): call("v", [V("q" + q, a, b), V("s" + q, a, b)], [t], lambda: g.vector.quantize_mx(ap(V("q" + q, a, b)), ap(V("s" + q, a, b)), ap(t)))
    def mm(bank, l, r):
        o = V("ps", 512 * bank, 512 * bank + r[0][2] - r[0][1])
        call("t", [o], list(l) + list(r), lambda: g.tensor.matmul_mx(ap(o), ap(l[0]), ap(l[1]), ap(r[0]), ap(r[1]), True, True))
        return o
    def mx(q, a, b): return (V("q" + q, a, b), V("s" + q, a, b))
    def iota(o, pat, base, cm):
        small = SCRATCH[o[0]][2] != "int32"
        call("g", [o], [], lambda: g.iota(ap(o), pat, base, cm, allow_small_or_imprecise_dtypes=True) if small else g.iota(ap(o), pat, base, cm))
    def select(o, i, pat, op, other, base, cm): call("g", [o], [i], lambda: g.affine_select(ap(o), ap(i), pat, op, float(other), base, cm))
    def trans(o, i): call("v", [o], [i], lambda: g.vector.transpose(ap(o), ap(i)))
    def col(name, j): return V(name, j, j + 1)
    def ones(o): return V("ones", 0, len(range(o[1], o[2], o[3])))
    def one(o, c): act(o, ones(o), c)
    def fill(o, c): select(o, ones(o), [[0, ones(o)[2]]], A.is_equal, c, 1, 0)
    def resets(o, n): select(o, ones(o), [[0, o[2] // n], [1, n]], A.not_equal, 0.0, 0, 0)
    def vec(n): return col("vc", n)

    def fixed():
        for at, i in ((1, 6), (3, 5), (5, 4), (9, 6), (11, 4)):
            yield fill(V("b0", 16 + at, 144, 32), F[i])
            yield fill(V("b0", 32 + at, 144, 32), F[i] / F[7])
        yield fill(V("b0", 31, 144, 32), 1.0)
        for at, i in ((B3, 3), (B2, 2), (B1, 1), (B0, 0)):
            yield fill(V("w", at, 128, 32), F[i] / F[7])
        for at, c in ((0, 0.0), (8, F[3]), (15, F[2]), (65, 0.0), (72, F[1]), (80, F[0])):
            yield fill(V("d12", at, 64 if at < 64 else 129, 16), c)

    def paint(runs):
        for run in runs:
            if len(run) == 2:
                yield act(V("rows", *run), V("rows", 128, 128 + run[1] - run[0]))
            else:
                o = V("rows", *run[:3])
                yield lin(o, V("s16", 0, ones(o)[2]), run[4], float(run[3]))

    def tables():
        yield act(col("pv", 13), col("pv", 8), -512.0)
        yield act(col("pv", 9), col("pv", 2), 32.0)
        yield lin(V("vc"), V("vecs", 15, 192, 16), 1.0, col("pv", 13))
        yield lin(V("qk"), V("qk"), 1.0, col("pv", 9))
        for n in range(3):
            yield lin(S("il", 4 * n, 4 * n + 4), V("q8", 0, 16, 4), 1.0, vec(2 * n))
            yield lin(S("kl", 4 * n, 4 * n + 4), V("q8", 0, 16, 4), 1.0, vec(2 * n + 1))
        yield act(S("il", 12, 13), vec(6))
        yield lin(S("kl", 12, 13), vec(6), 1.0, 1.0)
        for n in range(2):
            yield lin(S("gl", 4 * n, 4 * n + 4), V("q8", 0, 16, 4), 4.0, vec(7 + n))
        for j in range(2):
            yield lin(S("soon", j, 12, 2), V("rows", 129, 135), 1.0, col("qk", j))
            yield lin(S("soon", 12 + 2 * j, 14 + 2 * j), V("qk", 0, 2), 1.0, vec(10 + j))
            yield lin(S("late", 12 + 2 * j, 14 + 2 * j), V("qk", 0, 2), 1.0, float((W1, W0)[j]))
        yield lin(col("pv", 10), col("pv", 1), -32.0, 231.0)
        yield lin(S("late", 0, 12), V("qk", 0, 12), 1.0, vec(9))
        yield lin(col("pv", 12), col("pv", 2), 8.0, col("pv", 10))
        yield lin(S("posl"), V("q8"), 1.0, col("pv", 10))
        yield lin(S("mvl"), V("c2", 0, 16, 8), 1.0, col("pv", 12))

    def gaps():
        lin(col("pv", 14), col("pv", 8), 1.0, 0.5)
        one(V("gap", 1, 256, 2), 4.0)
        lin(col("pv", 15), col("pv", 8), 2.0, 1.0)
        lin(col("base", 2), col("pv", 8), -2.0, 1.0)
        act(col("base", 3), col("pv", 8), -1.0)
        for o, c in ((V("gap", 0, 256, 2), col("pv", 14)), (V("turn", 0, 256, 2), col("pv", 15)), (V("turn", 1, 256, 2), col("base", 2))):
            lin(o, ones(o), 0.0, c)

    def preparing(r):
        if roles[r]:
            w0, at = ("w0", 0) if r else ("snd0", 32)
            yield tt(V("dd", 0, 16), V("wd", 1, 32, 2), V("wd", 0, 32, 2), A.subtract)
            yield ts(V("tt"), V("dd", 0, 16), col("pv", 8), A.mult)
            yield tt(V(w0, at, at + 32, 2), V("wd", 0, 32, 2), V("tt"), A.subtract)
            yield tt(V(w0, at + 1, at + 32, 2), V("wd", 1, 32, 2), V("tt"), A.add)
            return
        yield tt(V("nei"), I(V("wd"), V("fast")), V("tslow"), A.not_equal)
        yield None
        yield scan(V("far"), V("nei"), V("gap"), A.mult, A.add)
        yield tt(V("sig"), V("nei", 0, 256, 2), V("nei", 1, 256, 2), A.subtract)
        yield cp(V("snd%d" % r, 32, 64), V("far", 7, 256, 8))
        yield scan(V("rsc"), V("nei"), V("turn"), A.mult, A.add)

    def early(r):
        send(T.cores[rank ^ STEPS[r]], V("lnd%d" % r, 32, 64), V("snd%d" % r, 32, 64), "a%d" % (9 + r), writes=r == 0 or not roles[r], gets=r == 0 or roles[r])

    def state_list():
        act(V("wd"), V("nw", 7, 256, 8))
        lin(col("base", 1), col("base", 0), 1.0, float(C))
        lin(col("base", 2), col("base", 0), -4096.0, 4096.0 * (NT - 0.5))
        lin(V("h3"), V("h1"), 1.0, col("base", 1))
        lin(V("h4"), V("h1"), -4096.0, col("base", 2))
        yield None
        yield tt(V("h4"), V("h4"), V("h3"), A.min)
        yield tt(V("h4"), V("h4"), V("tabn"), A.max)

    def weave(*chains):
        chains = list(chains)
        while chains:
            chains = [c for c in chains if next(c, 0) is None]

    def some(chain, n):
        for _ in range(n):
            next(chain, 0)

    roles = [rank < rank ^ s for s in STEPS]
    dma("s", ap(V("pi")), T.p[:], [V("pi")], [])
    dma("y", ap(V("ut")), T.u[:], [V("ut")], [])
    for a, e in X0:
        dma("y", ap(V("x0", 4 * a, 4 * e)), T.x[:, 4 * a:4 * e], [V("x0", 4 * a, 4 * e)], [])
    dma("y", ap(V("hi")), T.h[:], [V("hi")], [])

    iota(V("si", 0, 2), [[0, 2]], 0, 1)
    iota(V("s16", 0, 32), [[-1, 2], [1, 16]], 0, 0)
    iota(V("q8"), [[8, 4], [0, 4]], 0, 0)
    iota(V("ia", 0, 8), [[16, 8]], 0, 0)
    if not roles[0]:
        iota(V("tslow"), [[8, 4], [1, 8], [0, 8]], 0, 0)
    ms(V("ones"), 1.0)
    one(V("rows", 32, 96), 0.0)
    one(V("rows", 112, 136), NIL)
    one(V("stg"), 0.0)
    iota(V("rows", 0, 32), [[1, 2], [0, 4], [-1, 4]], 6, 0)
    iota(V("rows", 96, 112), [[-2, 2], [8, 4], [-1, 2]], 3, 0)
    iota(V("c2"), [[2, 16]], 0, 0)
    iota(V("qk"), [[0, 8], [64, 2]], 0, 0)
    iota(V("i64"), [[1, 64]], 0, 0)
    resets(V("rst4"), 4)
    if not all(roles):
        iota(V("kback"), [[0, 4], [-1, 8], [0, 8]], 8, 0)
    resets(V("rst8"), 8)
    ms(V("b0"), 0.0)
    ts(V("si", 2, 3), col("si", 0), 15, A.bitwise_and)
    ts(V("si", 3, 4), col("si", 0), 7, A.bitwise_and)
    ts(V("si", 4, 5), col("si", 0), 3, A.logical_shift_right, 1, A.bitwise_and)
    ts(V("si", 5, 6), col("si", 0), 4, A.logical_shift_right, 1, A.bitwise_and)
    ts(V("si", 6, 7), col("si", 0), 3, A.bitwise_and)
    ms(V("d12"), 1.0)
    cp(V("pv", 0, 5), V("si", 2, 7))
    ts(col("pv", 5), col("si", 5), -1.0, A.mult, 1.0, A.add)
    ts(col("pv", 8), col("si", 2), 15.0, A.is_lt, 2.0, A.mult)
    ms(V("et"), 0.0)
    rows = paint(PLACES + PAIRS)
    some(rows, 6)
    act(col("pv", 6), col("pv", 0), 32.0)
    lin(col("pv", 11), col("pv", 4), 16.0, 15.0)
    ts(V("s16", 32, 48), V("s16", 0, 16), col("pv", 0), A.is_equal, -4096.0, A.mult)
    ts(V("s16", 16, 32), V("s16", 16, 32), col("pv", 0), A.is_equal, 1024.0, A.mult)
    ts(V("rep"), V("ones", 0, 32), col("pv", 0), A.mult)
    tt(V("s16", 16, 32), V("s16", 16, 32), V("s16", 32, 48), A.add)
    for v in range(2):
        for e in range(2):
            ts(V("t64", 32 * v + 16 * e, 32 * v + 16 * e + 16), V("pi", v, 32, 2), col("pv", 5 - 2 * e), A.mult)
    ts(V("fast"), V("q8"), col("pv", 1), A.add)
    trans(V("u64"), V("t64"))
    cp(V("ul"), V("ia", 0, 8))
    for v in range(2):
        tt(V("opf", 16 * v, 16 * v + 16), V("u64", 32 * v, 32 * v + 16), V("u64", 32 * v + 16, 32 * v + 32), A.add)
    ts(V("wd"), V("opf"), col("pv", 6), A.subtract)
    if not all(roles):
        gaps()
    some(rows, ROWS_EARLY)
    act(V("selk"), I(V("s16", 16, 32), V("rep")))
    quant("u", V("ut"), 0, 128)
    ready = preparing(0)
    some(ready, 4 if roles[0] else 2)
    call("v", [V("qu2")], [I(V("qu"), V("ul"))], lambda: g.vector.tensor_copy(ap(V("qu2"), dt.uint32), ap(I(V("qu"), V("ul")), dt.uint32)))
    call("s", [V("su2")], [I(V("su"), V("ul"))], lambda: g.scalar.activation(ap(V("su2")), ap(I(V("su"), V("ul"))), AF.Copy))
    act(V("sel2"), V("selk", 0, 256), 2.0 ** -9)
    some(ready, 3)
    early(0)
    cp(V("al"), V("opf", 0, 32, 2))
    weights = fixed()
    some(weights, FIXED_EARLY)
    cp(V("bl"), V("opf", 1, 32, 2))
    weave(rows)
    lists = tables()
    ts(V("sgl"), V("q8", 0, 16, 2), 8.0, A.mult, col("pv", 11), A.add)
    if roles[0]:
        ts(V("dd", 16, 32), V("dd", 0, 16), -1.0, A.mult)
    for k, (a, e) in enumerate(X0):
        quant("x", V("x0", 4 * a, 4 * e), a, e)
        if k == 0:
            scan(V("vecs"), V("selk", 0, 192), V("rows"), A.add, A.max)
            some(lists, LISTS_EARLY)
            weave(ready)
        o = mm(k, mx("u2", 0, 128), mx("x", a, e))
        if e == C:
            cp(V("hn"), V("hi"))
            for b in range(4):
                ts(V("h0", 32 * b, 32 * b + 32), V("hi"), 4.0, A.mult, float(b), A.add)
        move("v" if e == C else "s", V("ssb", a, e), o)
    xcur = "x0"
    for r, step in enumerate(STEPS):
        peer = T.cores[rank ^ step]
        left = roles[r]
        last = r == len(STEPS) - 1
        snd, lnd, ahead = "snd%d" % r, V("lnd%d" % r, 0, 32), V("lnd%d" % r, 32, 64)

        def by_letter(b):
            act(V("xl", 512 * b, 512 * b + 512), I(V(xcur), V("h1l" if r else "h0", 32 * b, 32 * b + 32)))

        src = "ssb"
        if r == 0:
            src = "hsc"
            act(V(src, 0, 256), I(V("ssb"), V("hn", 0, 16)))
            cp(V(src, 256, 512), I(V("ssb"), V("hn", 16, 32)))
        act(V("bs", 128, 256), I(V(src), V("bl", 8, 16)))
        if r == 1:
            tt(V("hf"), V("hf"), V("ib"), A.add)
            for b in range(4):
                lin(V("h4b", 32 * b, 32 * b + 32), V("hf"), 4.0, float(b))
        elif r == 0:
            if not all(roles):
                lin(V("kback"), V("kback"), 1.0, col("base", 3))
            some(lists, LISTS_NEXT)
        if r and left:
            act(V("ob"), I(ahead, V("il", 0, 13)))
        if r > 1:
            by_letter(0)
        cp(V("bs", 0, 128), I(V(src), V("bl", 0, 8)))
        tt(V("fl"), I(V(src), V("al")), V("bs"), A.is_lt)
        if r == 1:
            cp(V("h1l"), V("h4b"))
            by_letter(0)
        scan(V("fsc"), V("sel2"), V("fl"), A.add, A.max)
        flags = V("fsc", 15, 256, 16)
        mine = snd if left and r else "r0"
        if left and r == 0:
            tt(V(snd, 0, 32, 2), flags, V("dd", 0, 16), A.mult)
            tt(V(snd, 1, 32, 2), flags, V("dd", 16, 32), A.mult)
        elif left:
            tt(V("tt"), flags, V("dd", 0, 16), A.mult)
            tt(V(snd, 0, 32, 2), V("w0", 0, 32, 2), V("tt"), A.add)
            tt(V(snd, 1, 32, 2), V("w0", 1, 32, 2), V("tt"), A.subtract)
        else:
            tt(V("sg1"), I(V("fsc"), V("sgl")), V("sig"), A.mult)
            scan(V("sg2"), V("rst4"), V("sg1"), A.mult, A.add)
            cp(V(snd, 0, 32), V("sg2", 3, 128, 4))
            tt(V(mine), V("sg2", 3, 128, 4), V("rsc", 7, 256, 8), A.add)
        send(peer, lnd, V(snd, 0, 32), "a%d" % (3 * r))
        if r == 0:
            dma("y", ap(V("qw"), dt.uint8), T.wc[:], [V("qw")], [lnd])
            dma("y", ap(V("sw")), T.ws[:], [V("sw")], [])
            dma("y", ap(V("vt")), T.v[:], [V("vt")], [])
            weave(weights)
            iota(V("itab"), [[0, 4], [1, 8]], 0, 0)
            if left:
                iota(V("kslow"), [[0, 4], [1, 8], [0, 8]], 0, 0)
            iota(V("iota"), [[1, 512]], 0, 0)
            cp(V("lists", 0, 32), V("stg", 0, 32))
            if left:
                tt(V(mine), V(snd, 32, 64), V(snd, 0, 32), A.add)
            iota(V("erow", 0, NT), [[0, NT]], 0, 0)
            iota(V("place"), [[1, 16], [16, 32]], 0, 0)
            select(V("et"), V("et"), [[-1, 528]], A.not_equal, 16.0, 3, 4)
            if left and not all(roles):
                iota(V("tslow"), [[8, 4], [1, 8], [0, 8]], 0, 0)
            if not left and any(roles):
                iota(V("kslow"), [[0, 4], [1, 8], [0, 8]], 0, 0)
        sign = -1.0 if left else 1.0
        act(V("m64"), V(mine, 0, 32), -64.0 * sign)
        lin(V("o1"), I(V(mine, 0, 32), V("il", 0, 13)), 64.0 * sign, 32.0 * sign)
        if left and r == 0:
            act(V("ob"), I(ahead, V("il", 0, 13)))
        if r == 0:
            weave(lists)
        if left:
            tt(V("df", 0, 31), V(mine, 0, 31), V(mine, 1, 32), A.subtract)
            if r:
                tt(V("x1"), I(ahead, V("kl", 0, 13)), V("ob"), A.subtract)
            cp(V("df", 7, 32, 8), V(mine, 7, 32, 8))
        else:
            tt(V("dtl"), I(V(mine, 0, 32), V("fast")), V("kback"), A.is_equal)
        if r == 0:
            ms(V("mlt", 0, 16), 0.0)
            ts(V("mlt", 16, 32), V("s16", 0, 16), col("pv", 0), A.is_lt)
        tt(V("own"), I(V("m64"), V("kl", 0, 13)), V("o1"), A.add)
        if r == 0:
            cp(V("lists", 32, 112), V("stg", 32, 112))
            if left:
                tt(V("x1"), I(ahead, V("kl", 0, 13)), V("ob"), A.subtract)
            else:
                tt(V("lv1"), ahead, lnd, A.add)
                lnd = V("lv1")
            by_letter(0)
        if left:
            tt(V("x1"), V("x1"), V("own"), A.min)
            act(V("dtl"), I(V("df"), V("fast")))
        else:
            for q in range(4):
                lin(V("dtl", 64 * q, 64 * q + 64), V("dtl", 64 * q, 64 * q + 64), 64.0, 8.0 * q - 64.0)
        if r == 0:
            lin(col("tabd", 32), col("pv", 6), 1.0, 511.0)
            lin(col("tabd", 33), col("pv", 6), 1.0, 543.0)
            lin(V("tabd", 0, 32), V("i64", 2, 34), 1.0, col("tabd", 32))
            act(col("pv", 7), col("pv", 8), 512.0)
        for b in range(1, 3 if r else 2):
            by_letter(b)

        def leads(o, a, e):
            tt(o, I(lnd, V("il" if left else "kl", a, e)), V("x1", 16 * a, 16 * e), A.is_ge if left else A.is_le)

        if not left:
            tt(V("x1", 0, 64), I(lnd, V("il", 0, 4)), V("own", 0, 64), A.max)
            tt(V("x1", 64, 208), I(lnd, V("il", 4, 13)), V("own", 64, 208), A.max)
        leads(V("b0", 16, 144, 2), 0, 4)
        leads(V("lg", 0, 64), 4, 8)
        scan(V("w", W7, 240), V("b0", 15, 128), V("b0", 31, 144), A.mult, A.max)
        leads(V("d12", 2, 130, 8), 12, 13)
        act(V("w", YES, 512, 32), V("d12", 74, 129, 16), HUGE)
        lin(V("w", NO, 512, 32), V("d12", 74, 129, 16), -HUGE, HUGE)
        tt(V("pp", 0, 64), I(V("w", 0, 256), V("gl", 0, 4)), V("lg", 0, 64), A.mult)
        leads(V("lg", 64, 128), 8, 12)
        scan(V("w", 256, 384, 2), V("d12", 0, 64), V("pp", 0, 64), A.mult, A.max)
        act(V("wi", 192, 256), I(V("w", 0, 512), V("soon", 12, 16)))
        act(V("wi", 0, 192), I(V("w", 0, 512), V("soon", 0, 12)))
        for b in range(3 if r else 2, 4):
            by_letter(b)
        tt(V("pp", 64, 128), I(V("w", 0, 384), V("gl", 4, 8)), V("lg", 64, 128), A.mult)
        scan(V("w", 512, 640, 2), V("d12", 65, 129), V("pp", 64, 128), A.mult, A.max)
        tt(V("cmp", 192, 256), I(V("w"), V("late", 12, 16)), V("wi", 192, 256), A.is_lt)
        tt(V("cmp", 0, 192), I(V("w"), V("late", 0, 12)), V("wi", 0, 192), A.is_gt)
        scan(V("pos"), V("rst8"), V("cmp"), A.mult, A.add)

        outs = {}
        steps = {
            "mv": lambda: tt(V("mv"), I(V("pos"), V("mvl")), V("itab"), A.not_equal),
            "cc": lambda: scan(V("cc"), V("ones", 0, 32), V("mv"), A.add, A.add, col("tabd", 32)),
            "ha": lambda: tt(V("h1"), V("mv"), V("tabd", 0, 32), A.mult),
            "hb": lambda: tt(V("h1"), V("cc"), V("h1"), A.subtract),
            "tot": lambda: ts(V("tot"), V("cc", 30, 32), col("tabd", 33), A.subtract),
            "tr": lambda: tt(V("tr"), I(V("i64"), V("tot")), V("mlt"), A.mult),
            "base": lambda: call("v", [col("base", 0)], [V("tr")], lambda: g.vector.tensor_reduce(ap(col("base", 0)), ap(V("tr")), AxisListType.X, A.add)),
            "dst": lambda: ts(V("dst"), V("h1"), col("base", 0), A.add),
            "sc": lambda: cp(I(V("erow"), V("dst")), V("iota")),
            "esc": lambda: scan(V("esc"), V("selk", 0, NT), V("erow", 0, NT), A.add, A.max),
            "el": lambda: ts(V("el"), V("esc", 15, NT, 16), col("pv", 7), A.subtract),
        }
        for w in LPLAN:
            if w in steps:
                steps[w]()
            elif w[:2] in ("ne", "nw", "zl"):
                k = int(w[2])
                ne, nw, dtl, kslow, rst8 = [V(n, 128 * k, 128 * k + 128) for n in ("ne", "nw", "dtl", "kslow", "rst8")]
                if w[:2] == "ne":
                    tt(ne, I(V("pos"), V("posl", 8 * k, 8 * k + 8)), kslow if left else dtl, A.not_equal if left else A.add)
                elif w[:2] == "nw":
                    scan(nw, ne if left else rst8, dtl if left else ne, A.mult, A.add if left else A.max)
                else:
                    ts(V("zl", 16 * k, 16 * k + 16), V("nw", 128 * k + 7, 128 * k + 128, 8), col("pv", 6), A.add)
            elif w[0] == "q":
                k = int(w[1])
                quant("z", V("z", 1024 * k, 1024 * k + 1024), 256 * k, 256 * k + 256)
                outs[k] = [mm(4 * k + n, mx("w", 128 * n, 128 * n + 128), mx("z", 256 * k, 256 * k + 256)) for n in range(4)]
            elif w[0] == "f":
                b, c0, c1 = int(w[2]), int(w[3], 16), int(w[4], 16)
                move(w[1], V("ft", 64 * c0 + b, 64 * c1, 4), I(V("yg", YW * b, YW * b + C), V("el", c0, c1)), 2.0 ** -5)
            else:
                k, b = int(w[-2]), int(w[-1])
                z, z32 = V("z", 1024 * k + b, 1024 * k + 1024, 4), V("z32", 512 * b + 256 * k, 512 * b + 256 * k + 256)
                if w[0] == "g":
                    move(w[1], z, I(V("xl", 512 * b, 512 * b + 512), V("zl", 16 * k, 16 * k + 16)))
                elif w[0] == "z":
                    move(w[1], z32, z, 32.0)
                else:
                    tt(V("yg", YW * b + 256 * k, YW * b + 256 * k + 256), outs[k][b], z32, A.add)
        quant("f%d" % r, V("ft"), 0, NT)
        send(peer, V("lq%d" % r), V("qf%d" % r), "a%d" % (3 * r + 1), dt.uint8)
        send(peer, V("ls%d" % r), V("sf%d" % r), "a%d" % (3 * r + 2))
        if r == 0:
            lin(V("tabn"), V("i64", 0, 32), 16.0, col("pv", 0))
            act(V("hrow"), I(V("place"), V("hn")))
            for b in range(4):
                quant("e", V("et", 3 - b, 515 - b), 128 * b, 128 * b + 128)
        later = state_list()
        next(later)
        if not last:
            act(V("hw"), I(V("hrow"), V("zl")))
        act(V("f16"), V("ft"), 16.0)
        if not last:
            weave(preparing(r + 1), later)
            cp(V("xll"), V("h4"))
            scan(V("hsc"), V("selk"), V("hw"), A.add, A.max)
        else:
            weave(later)
            for v in range(2):
                for e in range(2):
                    ts(V("t64", 32 * v + 16 * e, 32 * v + 16 * e + 16), V("h4", 16 * v, 16 * v + 16), col("pv", 5 - 2 * e), A.mult)
            ts(V("opf"), V("wd"), col("pv", 6), A.add)
            trans(V("u64"), V("t64"))
            quant("v", V("vt"), 0, 128)
            for v in range(2):
                tt(V("h3", v, 32, 2), V("u64", 32 * v, 32 * v + 16), V("u64", 32 * v + 16, 32 * v + 32), A.add)
            cp(V("xll"), V("h3"))
            dma("y", T.op[:], ap(V("opf")), [], [V("opf")])
        for b in range(4):
            o = mm(4 + b, mx("e", 128 * b, 128 * b + 128), (V("lq%d" % r), V("ls%d" % r)))
            if b == 0 and not last:
                ts(V("al"), V("hsc", 15, 512, 32), col("pv", 7), A.subtract)
                ts(V("bl"), V("hsc", 31, 512, 32), col("pv", 7), A.subtract)
            tt(V("yg", YW * b + C, YW * b + YW), o, V("f16", b, 4 * NT, 4), A.add)
        if not last:
            order("g", [], [V("ls%d" % r)], ("sent", 0))
            early(r + 1)
        xcur = "xa"
        bank, after = 0, []
        for q, a, e, b in XLAST if last else XPLAN:
            if q != "q":
                move(q, V(xcur, 4 * a + b, 4 * e, 4), I(V("yg", YW * b, YW * b + YW), V("xll", a // 16, e // 16)), 2.0 ** -5)
                continue
            quant("x", V(xcur, 4 * a, 4 * e), a, e)
            if last:
                dma("y", T.oc[:, 4 * a:4 * e], ap(V("qx", a, e), dt.uint8), [], [V("qx", a, e)])
            after.append((a, e, b, mm(bank, mx("v" if last else "u2", 0, 128), mx("x", a, e))))
            bank += 1
        if r == 0:
            ts(V("ia"), V("hi"), 31, A.bitwise_and)
            ts(V("ib"), V("hi"), 5, A.logical_shift_right)
            ts(V("hf"), V("ia"), 16.0, A.mult)
        for a, e, q, o in after:
            if last and e == C:
                for k in range(4):
                    dma("ys"[k % 2], T.osc[4 * k:4 * k + 4, :], T.sx[32 * k:32 * k + 4, :], [], [V("sx")])
            move(q, V("yo" if last else "ssb", a, e), o)
            if last:
                dma("s", T.y[:, a:e], ap(V("yo", a, e)), [], [V("yo", a, e)])

    for s in sorted(total, key=lambda s: int(s[1:]) if s[0] == "d" else -1):
        wait("g", (s, total[s]))
